import numpy as np
import ml_dtypes


def mxq(x, axis, fmt="e4m3"):
    dtype, down = {"e4m3": (ml_dtypes.float8_e4m3fn, 7), "e5m2": (ml_dtypes.float8_e5m2, 14)}[fmt]
    v = np.moveaxis(np.asarray(x, np.float32).astype(ml_dtypes.bfloat16).astype(np.float64), axis, -1)
    blocks = v.reshape(v.shape[:-1] + (-1, 32))
    amax = np.abs(blocks).max(-1, keepdims=True)
    byte = np.maximum(np.where(amax > 0, np.frexp(amax)[1] - 1 + 127, 0) - down, 1)
    scale = np.exp2(byte - 127.0)
    codes = (blocks / scale).astype(np.float32).astype(dtype).astype(np.float64)
    return np.moveaxis((codes * scale).reshape(v.shape), -1, axis)


WIDE = False


def mx_kscale(k):
    if not WIDE:
        return np.ones(k)
    levels = np.array([10, -10, 5, -5, 0])
    if k % 512:
        return np.exp2(np.random.permutation(np.resize(levels, k // 32))).repeat(32)
    a = np.empty((k // 512, 16))
    for p in range(k // 512):
        a[p, :8] = np.random.permutation(np.resize(levels, 8))
        for g in range(8):
            far = levels[np.abs(levels - a[p, g]) >= 10]
            a[p, g + 8] = far[np.random.randint(len(far))]
    return np.exp2(a.ravel()).repeat(32)


def f64(x):
    return np.asarray(x).astype(np.float64)


def striped(idx):
    return np.tile(idx.reshape(-1, 16).T, (8, 1)).astype(np.uint16)


def unstriped(offs):
    return offs[:16].T.reshape(-1).astype(np.int64)


def silu(v):
    return v / (1.0 + np.exp(-np.maximum(v, -700.0)))


K, T, E, C, H, N = 512, 2048, 8, 256, 512, 512


def by_expert(wq, xq):
    return np.concatenate([wq[e].T @ xq[:, e * C:(e + 1) * C] for e in range(E)], axis=1)


def setup_inputs():
    n = np.random.standard_normal
    s = mx_kscale(K)[:, None]
    u = mx_kscale(H)
    return {
        "xT": (n((K, T)) * s).astype(np.float32),
        "w1": (n((E, K, H)) / np.sqrt(K) / s[None] * u[None, None, :]).astype(np.float32),
        "w2": (n((E, H, N)) / np.sqrt(H) / u[None, :, None]).astype(np.float32),
        "gate": np.tile(np.random.uniform(0.2, 1.0, E * C), (N, 1)).astype(np.float32),
        "offs": striped(np.random.permutation(T)[:E * C]),
    }


def reference(xT, w1, w2, gate, offs):
    idx = unstriped(offs)
    xq = mxq(f64(xT)[:, idx], 0, "e4m3")
    h = silu(by_expert(mxq(f64(w1), 1, "e4m3"), xq))
    y = by_expert(mxq(f64(w2), 1, "e4m3"), mxq(h, 0, "e4m3"))
    out = np.zeros((N, T))
    out[:, idx] = f64(gate) * y
    return out

@@ -1,0 +1,216 @@
+from contextlib import ExitStack
+
+import concourse.mybir as mybir
+
+K, T, E, C, H, N = 512, 2048, 8, 256, 512, 512
+FLOPS = 2 * E * C * (K * H + H * N)
+
+F32 = mybir.dt.float32
+BF16 = mybir.dt.bfloat16
+U32 = mybir.dt.uint32
+U16 = mybir.dt.uint16
+U8 = mybir.dt.uint8
+FP8X4 = mybir.dt.float8_e4m3fn_x4
+SILU = mybir.ActivationFunctionType.Silu
+MULT = mybir.AluOpType.mult
+
+P = 128
+XW = 512
+XCH = T // XW
+GS = 512
+NS = E * C // GS
+HALF = 128
+NB = N // P
+FORM = "d"
+V_IL = ()
+G_IL = ()
+FAST = True
+
+
+def tile_routed_moe_kernel(tc, xT, w1, w2, gate, offs, out):
+    nc = tc.nc
+    with ExitStack() as ctx:
+        keep = ctx.enter_context(tc.tile_pool(name="keep", bufs=1))
+        wraw_pool = ctx.enter_context(tc.tile_pool(name="wraw_pool", bufs=5))
+        wg_pool = ctx.enter_context(tc.tile_pool(name="wg_pool", bufs=3))
+        wq_pool = ctx.enter_context(tc.tile_pool(name="wq_pool", bufs=3))
+        h_pool = ctx.enter_context(tc.tile_pool(name="h_pool", bufs=3))
+        y_pool = ctx.enter_context(tc.tile_pool(name="y_pool", bufs=3))
+        ps_pool = ctx.enter_context(tc.psum_pool(name="ps_pool", bufs=2))
+
+        offsets = keep.tile([P, E * C // 16], U16, name="offsets")
+        nc.sync.dma_start(offsets[:], offs)
+
+        warm_in = keep.tile([P, 1], F32, name="warm_in")
+        warm_out = keep.tile([P, 1], F32, name="warm_out")
+        nc.gpsimd.memset(warm_in[:], 0.0)
+        nc.scalar.activation(out=warm_out[:], in_=warm_in[:], func=SILU)
+
+        x_view = xT.rearrange("(p t) n -> p t n", t=4)
+        xraw = {}
+        for u in range(2):
+            for c in range(XCH):
+                xraw[(u, c)] = keep.tile([P, 2, XW], F32, name="xraw%d_%d" % (u, c))
+                nc.sync.dma_start(out=xraw[(u, c)][:], in_=x_view[:, 2 * u : 2 * u + 2, c * XW : (c + 1) * XW])
+
+        wraw = {}
+
+        def load_weights(e):
+            for layer, w in ((1, w1), (2, w2)):
+                wraw[(layer, e)] = wraw_pool.tile([P, 4, 512], F32, name="wraw")
+                nc.sync.dma_start(out=wraw[(layer, e)][:], in_=w[e, :, :].rearrange("(p j) c -> p j c", j=4))
+
+        load_weights(0)
+        gate_sb = keep.tile([P, E * C], F32, name="gate_sb")
+        nc.sync.dma_start(out=gate_sb[:], in_=gate[0:P, :])
+        for e in range(1, 2):
+            load_weights(e)
+
+        pairs = keep.tile([P, 2, T, 2], BF16, name="pairs")
+        for u in range(2):
+            for c in range(XCH):
+                dst = pairs[:, u, c * XW : (c + 1) * XW, :]
+                src = xraw[(u, c)][:].rearrange("p e n -> p n e")
+                if u == 0:
+                    nc.vector.tensor_copy(out=dst, in_=src)
+                else:
+                    nc.scalar.copy(out=dst, in_=src)
+
+        xg = [keep.tile([P, GS, 4], BF16, name="xg%d" % s, align_bytes=64) for s in range(NS)]
+        xc = [keep.tile([P, GS], U32, name="xc%d" % s, align_bytes=64) for s in range(NS)]
+        xs = [keep.tile([P, GS], U8, name="xs%d" % s, align_bytes=64) for s in range(NS)]
+
+        def gather(u, s):
+            window = pairs[:, u, :, :].rearrange("p n e -> p (n e)").bitcast(U32)
+            words = xg[s][:].rearrange("p n t -> p (n t)").bitcast(U32).rearrange("p (n u) -> p n u", u=2)
+            nc.vector.tensor_copy(
+                out=words[:, :, u],
+                in_=window.indirect(offsets[:, s * GS // 16 : (s + 1) * GS // 16]),
+            )
+
+        def quantize_tokens(s):
+            nc.vector.quantize_mx(
+                out=xc[s][:].bitcast(FP8X4),
+                scales=xs[s][:],
+                in_=xg[s][:].rearrange("p n t -> p (n t)"),
+            )
+
+        wq = {}
+
+        def prepare_weights(e):
+            for layer in (1, 2):
+                raw = wraw[(layer, e)]
+                grouped = wg_pool.tile([P, 4 * 512], BF16, name="grouped", align_bytes=64)
+                if layer == 1:
+                    if FAST:
+                        dst = grouped[:].rearrange("p (t m j) -> p m j t", t=4, j=4)
+                        src = raw[:].rearrange("p j (m t) -> p m j t", t=4)
+                    else:
+                        dst = grouped[:].rearrange("p (t m j) -> p t m j", t=4, j=4)
+                        src = raw[:].rearrange("p j (m t) -> p t m j", t=4)
+                else:
+                    if FAST:
+                        dst = grouped[:].rearrange("p (c i j) -> p c j i", i=4, j=4)
+                        src = raw[:].rearrange("p j (c i) -> p c j i", i=4)
+                    else:
+                        dst = grouped[:].rearrange("p (c j) -> p c j", j=4)
+                        src = raw[:].rearrange("p j c -> p c j")
+                if (layer, e) in V_IL:
+                    nc.vector.tensor_copy(out=dst, in_=src)
+                elif (layer, e) in G_IL:
+                    nc.gpsimd.tensor_scalar(dst, src, 1.0, 0.0, MULT, mybir.AluOpType.add)
+                else:
+                    nc.scalar.copy(out=dst, in_=src)
+                codes = wq_pool.tile([P, 512], U32, name="codes%d" % layer, align_bytes=64)
+                scales = wq_pool.tile([P, 512], U8, name="scales%d" % layer, align_bytes=64)
+                nc.vector.quantize_mx(out=codes[:].bitcast(FP8X4), scales=scales[:], in_=grouped[:])
+                wq[(layer, e)] = (codes, scales)
+
+        out_sb = [keep.tile([P, T], F32, name="out_sb%d" % nb) for nb in range(NB)]
+        staged = {}
+
+        hq = {}
+
+        def first_layer(e):
+            s, col = (e * C) // GS, (e * C) % GS
+            c1, s1 = wq[(1, e)]
+            hg = h_pool.tile([P, C, 4], BF16, name="hg", align_bytes=64)
+            for half in range(C // HALF):
+                lo = col + half * HALF
+                ps1 = ps_pool.tile([P, 4, HALF], F32, name="bank")
+                for t in range(4):
+                    nc.tensor.matmul_mx(
+                        out=ps1[:, t, :],
+                        lhsT=c1[:, t * P : (t + 1) * P].bitcast(FP8X4),
+                        lhsT_scale=s1[:, t * P : (t + 1) * P],
+                        rhs=xc[s][:, lo : lo + HALF].bitcast(FP8X4),
+                        rhs_scale=xs[s][:, lo : lo + HALF],
+                        start=True,
+                        stop=True,
+                    )
+                nc.scalar.activation(
+                    out=hg[:, half * HALF : (half + 1) * HALF, :],
+                    in_=ps1[:].rearrange("p t n -> p n t"),
+                    func=SILU,
+                )
+            hc = h_pool.tile([P, C], U32, name="hc", align_bytes=64)
+            hs = h_pool.tile([P, C], U8, name="hs", align_bytes=64)
+            nc.vector.quantize_mx(out=hc[:].bitcast(FP8X4), scales=hs[:], in_=hg[:].rearrange("p n t -> p (n t)"))
+            hq[e] = (hc, hs)
+
+        def second_layer(e):
+            c2, s2 = wq[(2, e)]
+            hc, hs = hq[e]
+            y = y_pool.tile([P, NB, C], F32, name="y")
+            for q in range(NB // 2):
+                ps2 = ps_pool.tile([P, 2, C], F32, name="bank")
+                for i in range(2):
+                    nb = 2 * q + i
+                    nc.tensor.matmul_mx(
+                        out=ps2[:, i, :],
+                        lhsT=c2[:, nb * P : (nb + 1) * P].bitcast(FP8X4),
+                        lhsT_scale=s2[:, nb * P : (nb + 1) * P],
+                        rhs=hc[:].bitcast(FP8X4),
+                        rhs_scale=hs[:],
+                        start=True,
+                        stop=True,
+                    )
+                if FORM == "d":
+                    nc.scalar.copy(out=y[:, 2 * q : 2 * q + 2, :], in_=ps2[:])
+                else:
+                    nc.vector.tensor_tensor(
+                        y[:, 2 * q : 2 * q + 2, :],
+                        ps2[:],
+                        gate_sb[:, e * C : (e + 1) * C].unsqueeze(1).to_broadcast([P, 2, C]),
+                        MULT,
+                    )
+            staged[e] = y
+
+        def way_back(e):
+            for nb in range(NB):
+                window = out_sb[nb][:].indirect(offsets[:, e * C // 16 : (e + 1) * C // 16])
+                if FORM == "d":
+                    nc.vector.tensor_tensor(window, staged[e][:, nb, :], gate_sb[:, e * C : (e + 1) * C], MULT)
+                else:
+                    nc.vector.tensor_copy(out=window, in_=staged[e][:, nb, :])
+                if e == E - 1:
+                    nc.sync.dma_start(out=out[nb * P : (nb + 1) * P, :], in_=out_sb[nb][:])
+
+        for s in range(NS):
+            gather(0, s)
+        gather(1, 0)
+        quantize_tokens(0)
+        prepare_weights(0)
+        prepare_weights(1)
+        first_layer(0)
+        for e in range(E):
+            if e % 2 == 0 and e // 2 + 1 < NS:
+                gather(1, e // 2 + 1)
+                quantize_tokens(e // 2 + 1)
+            if e + 1 < E:
+                first_layer(e + 1)
+            second_layer(e)
+            if e + 2 < E:
+                load_weights(e + 2)
+                prepare_weights(e + 2)
+            way_back(e)

@@ -21,10 +21,9 @@ GS = 512
 NS = E * C // GS
 HALF = 128
 NB = N // P
-FORM = "d"
-V_IL = ()
+GA = 512
+V_IL = ((2, 0), (2, 1),)
 G_IL = ()
-FAST = True
 
 
 def tile_routed_moe_kernel(tc, xT, w1, w2, gate, offs, out):
@@ -48,23 +47,33 @@ def tile_routed_moe_kernel(tc, xT, w1, w2, gate, offs, out):
 
         x_view = xT.rearrange("(p t) n -> p t n", t=4)
         xraw = {}
-        for u in range(2):
-            for c in range(XCH):
-                xraw[(u, c)] = keep.tile([P, 2, XW], F32, name="xraw%d_%d" % (u, c))
-                nc.sync.dma_start(out=xraw[(u, c)][:], in_=x_view[:, 2 * u : 2 * u + 2, c * XW : (c + 1) * XW])
+
+        def load_x(u, c):
+            xraw[(u, c)] = keep.tile([P, 2, XW], F32, name="xraw%d_%d" % (u, c))
+            nc.sync.dma_start(out=xraw[(u, c)][:], in_=x_view[:, 2 * u : 2 * u + 2, c * XW : (c + 1) * XW])
 
         wraw = {}
 
-        def load_weights(e):
-            for layer, w in ((1, w1), (2, w2)):
-                wraw[(layer, e)] = wraw_pool.tile([P, 4, 512], F32, name="wraw")
-                nc.sync.dma_start(out=wraw[(layer, e)][:], in_=w[e, :, :].rearrange("(p j) c -> p j c", j=4))
+        def load_weight(layer, e):
+            if (layer, e) in wraw:
+                return
+            w = w1 if layer == 1 else w2
+            wraw[(layer, e)] = wraw_pool.tile([P, 4, 512], F32, name="wraw")
+            nc.sync.dma_start(out=wraw[(layer, e)][:], in_=w[e, :, :].rearrange("(p j) c -> p j c", j=4))
 
-        load_weights(0)
+        def load_weights(e):
+            load_weight(1, e)
+            load_weight(2, e)
+
         gate_sb = keep.tile([P, E * C], F32, name="gate_sb")
+        for u in range(2):
+            for c in range(XCH):
+                load_x(u, c)
+        load_weight(1, 0)
+        load_weight(2, 0)
         nc.sync.dma_start(out=gate_sb[:], in_=gate[0:P, :])
-        for e in range(1, 2):
-            load_weights(e)
+        load_weight(1, 1)
+        load_weight(2, 1)
 
         pairs = keep.tile([P, 2, T, 2], BF16, name="pairs")
         for u in range(2):
@@ -77,8 +86,9 @@ def tile_routed_moe_kernel(tc, xT, w1, w2, gate, offs, out):
                     nc.scalar.copy(out=dst, in_=src)
 
         xg = [keep.tile([P, GS, 4], BF16, name="xg%d" % s, align_bytes=64) for s in range(NS)]
-        xc = [keep.tile([P, GS], U32, name="xc%d" % s, align_bytes=64) for s in range(NS)]
-        xs = [keep.tile([P, GS], U8, name="xs%d" % s, align_bytes=64) for s in range(NS)]
+        xq_pool = ctx.enter_context(tc.tile_pool(name="xq_pool", bufs=1))
+        xc = {}
+        xs = {}
 
         def gather(u, s):
             window = pairs[:, u, :, :].rearrange("p n e -> p (n e)").bitcast(U32)
@@ -89,6 +99,8 @@ def tile_routed_moe_kernel(tc, xT, w1, w2, gate, offs, out):
             )
 
         def quantize_tokens(s):
+            xc[s] = xq_pool.tile([P, GS], U32, name="xc", align_bytes=64)
+            xs[s] = xq_pool.tile([P, GS], U8, name="xs", align_bytes=64)
             nc.vector.quantize_mx(
                 out=xc[s][:].bitcast(FP8X4),
                 scales=xs[s][:],
@@ -102,19 +114,11 @@ def tile_routed_moe_kernel(tc, xT, w1, w2, gate, offs, out):
                 raw = wraw[(layer, e)]
                 grouped = wg_pool.tile([P, 4 * 512], BF16, name="grouped", align_bytes=64)
                 if layer == 1:
-                    if FAST:
-                        dst = grouped[:].rearrange("p (t m j) -> p m j t", t=4, j=4)
-                        src = raw[:].rearrange("p j (m t) -> p m j t", t=4)
-                    else:
-                        dst = grouped[:].rearrange("p (t m j) -> p t m j", t=4, j=4)
-                        src = raw[:].rearrange("p j (m t) -> p t m j", t=4)
+                    dst = grouped[:].rearrange("p (t m j) -> p m j t", t=4, j=4)
+                    src = raw[:].rearrange("p j (m t) -> p m j t", t=4)
                 else:
-                    if FAST:
-                        dst = grouped[:].rearrange("p (c i j) -> p c j i", i=4, j=4)
-                        src = raw[:].rearrange("p j (c i) -> p c j i", i=4)
-                    else:
-                        dst = grouped[:].rearrange("p (c j) -> p c j", j=4)
-                        src = raw[:].rearrange("p j c -> p c j")
+                    dst = grouped[:].rearrange("p (c i j) -> p c j i", i=4, j=4)
+                    src = raw[:].rearrange("p j (c i) -> p c j i", i=4)
                 if (layer, e) in V_IL:
                     nc.vector.tensor_copy(out=dst, in_=src)
                 elif (layer, e) in G_IL:
@@ -128,7 +132,6 @@ def tile_routed_moe_kernel(tc, xT, w1, w2, gate, offs, out):
 
         out_sb = [keep.tile([P, T], F32, name="out_sb%d" % nb) for nb in range(NB)]
         staged = {}
-
         hq = {}
 
         def first_layer(e):
@@ -175,24 +178,13 @@ def tile_routed_moe_kernel(tc, xT, w1, w2, gate, offs, out):
                         start=True,
                         stop=True,
                     )
-                if FORM == "d":
-                    nc.scalar.copy(out=y[:, 2 * q : 2 * q + 2, :], in_=ps2[:])
-                else:
-                    nc.vector.tensor_tensor(
-                        y[:, 2 * q : 2 * q + 2, :],
-                        ps2[:],
-                        gate_sb[:, e * C : (e + 1) * C].unsqueeze(1).to_broadcast([P, 2, C]),
-                        MULT,
-                    )
+                nc.scalar.copy(out=y[:, 2 * q : 2 * q + 2, :], in_=ps2[:])
             staged[e] = y
 
         def way_back(e):
             for nb in range(NB):
                 window = out_sb[nb][:].indirect(offsets[:, e * C // 16 : (e + 1) * C // 16])
-                if FORM == "d":
-                    nc.vector.tensor_tensor(window, staged[e][:, nb, :], gate_sb[:, e * C : (e + 1) * C], MULT)
-                else:
-                    nc.vector.tensor_copy(out=window, in_=staged[e][:, nb, :])
+                nc.vector.tensor_tensor(window, staged[e][:, nb, :], gate_sb[:, e * C : (e + 1) * C], MULT)
                 if e == E - 1:
                     nc.sync.dma_start(out=out[nb * P : (nb + 1) * P, :], in_=out_sb[nb][:])
 

@@ -161,32 +161,58 @@ def tile_routed_moe_kernel(tc, xT, w1, w2, gate, offs, out):
             nc.vector.quantize_mx(out=hc[:].bitcast(FP8X4), scales=hs[:], in_=hg[:].rearrange("p n t -> p (n t)"))
             hq[e] = (hc, hs)
 
+        def second_layer_bank(blocks, dst):
+            ps2 = ps_pool.tile([P, 2, C], F32, name="bank")
+            for i, (e, nb) in enumerate(blocks):
+                c2, s2 = wq[(2, e)]
+                hc, hs = hq[e]
+                nc.tensor.matmul_mx(
+                    out=ps2[:, i, :],
+                    lhsT=c2[:, nb * P : (nb + 1) * P].bitcast(FP8X4),
+                    lhsT_scale=s2[:, nb * P : (nb + 1) * P],
+                    rhs=hc[:].bitcast(FP8X4),
+                    rhs_scale=hs[:],
+                    start=True,
+                    stop=True,
+                )
+            nc.scalar.copy(out=dst, in_=ps2[:])
+
         def second_layer(e):
-            c2, s2 = wq[(2, e)]
-            hc, hs = hq[e]
             y = y_pool.tile([P, NB, C], F32, name="y")
             for q in range(NB // 2):
-                ps2 = ps_pool.tile([P, 2, C], F32, name="bank")
-                for i in range(2):
-                    nb = 2 * q + i
-                    nc.tensor.matmul_mx(
-                        out=ps2[:, i, :],
-                        lhsT=c2[:, nb * P : (nb + 1) * P].bitcast(FP8X4),
-                        lhsT_scale=s2[:, nb * P : (nb + 1) * P],
-                        rhs=hc[:].bitcast(FP8X4),
-                        rhs_scale=hs[:],
-                        start=True,
-                        stop=True,
-                    )
-                nc.scalar.copy(out=y[:, 2 * q : 2 * q + 2, :], in_=ps2[:])
+                second_layer_bank([(e, 2 * q), (e, 2 * q + 1)], y[:, 2 * q : 2 * q + 2, :])
             staged[e] = y
+
+        def scatter(nb, sums, e, n_experts):
+            lo, hi = e * C, (e + n_experts) * C
+            window = out_sb[nb][:].indirect(offsets[:, lo // 16 : hi // 16])
+            nc.vector.tensor_tensor(window, sums, gate_sb[:, lo:hi], MULT)
+
+        def store(nb):
+            nc.sync.dma_start(out=out[nb * P : (nb + 1) * P, :], in_=out_sb[nb][:])
 
         def way_back(e):
             for nb in range(NB):
-                window = out_sb[nb][:].indirect(offsets[:, e * C // 16 : (e + 1) * C // 16])
-                nc.vector.tensor_tensor(window, staged[e][:, nb, :], gate_sb[:, e * C : (e + 1) * C], MULT)
-                if e == E - 1:
-                    nc.sync.dma_start(out=out[nb * P : (nb + 1) * P, :], in_=out_sb[nb][:])
+                scatter(nb, staged[e][:, nb, :], e, 1)
+
+        def last_two_experts():
+            a, b = E - 2, E - 1
+            ya = y_pool.tile([P, NB, C], F32, name="y")
+            yb = y_pool.tile([P, NB, C], F32, name="y")
+            second_layer_bank([(a, 0), (a, 1)], ya[:, 0:2, :])
+            second_layer_bank([(b, 0), (b, 1)], yb[:, 0:2, :])
+            second_layer_bank([(a, 2), (b, 2)], ya[:, 2:4, :])
+            second_layer_bank([(a, 3), (b, 3)], yb[:, 2:4, :])
+            scatter(0, ya[:, 0, :], a, 1)
+            scatter(1, ya[:, 1, :], a, 1)
+            scatter(0, yb[:, 0, :], b, 1)
+            store(0)
+            scatter(1, yb[:, 1, :], b, 1)
+            store(1)
+            scatter(2, ya[:, 2:4, :].rearrange("p a c -> p (a c)"), a, 2)
+            store(2)
+            scatter(3, yb[:, 2:4, :].rearrange("p a c -> p (a c)"), a, 2)
+            store(3)
 
         for s in range(NS):
             gather(0, s)
@@ -195,14 +221,14 @@ def tile_routed_moe_kernel(tc, xT, w1, w2, gate, offs, out):
         prepare_weights(0)
         prepare_weights(1)
         first_layer(0)
-        for e in range(E):
+        for e in range(E - 2):
             if e % 2 == 0 and e // 2 + 1 < NS:
                 gather(1, e // 2 + 1)
                 quantize_tokens(e // 2 + 1)
-            if e + 1 < E:
-                first_layer(e + 1)
+            first_layer(e + 1)
             second_layer(e)
-            if e + 2 < E:
-                load_weights(e + 2)
-                prepare_weights(e + 2)
+            load_weights(e + 2)
+            prepare_weights(e + 2)
             way_back(e)
+        first_layer(E - 1)
+        last_two_experts()

@@ -66,10 +66,10 @@ def tile_routed_moe_kernel(tc, xT, w1, w2, gate, offs, out):
             load_weight(2, e)
 
         gate_sb = keep.tile([P, E * C], F32, name="gate_sb")
+        load_weight(1, 0)
         for u in range(2):
             for c in range(XCH):
                 load_x(u, c)
-        load_weight(1, 0)
         load_weight(2, 0)
         nc.sync.dma_start(out=gate_sb[:], in_=gate[0:P, :])
         load_weight(1, 1)

@@ -22,7 +22,7 @@ NS = E * C // GS
 HALF = 128
 NB = N // P
 GA = 512
-V_IL = ((2, 0), (2, 1),)
+V_IL = ((2, 1),)
 G_IL = ()
 
 
@@ -71,8 +71,8 @@ def tile_routed_moe_kernel(tc, xT, w1, w2, gate, offs, out):
             for c in range(XCH):
                 load_x(u, c)
         load_weight(2, 0)
-        nc.sync.dma_start(out=gate_sb[:], in_=gate[0:P, :])
         load_weight(1, 1)
+        nc.sync.dma_start(out=gate_sb[:], in_=gate[0:P, :])
         load_weight(2, 1)
 
         pairs = keep.tile([P, 2, T, 2], BF16, name="pairs")

@@ -17,8 +17,9 @@ MULT = mybir.AluOpType.mult
 P = 128
 XW = 512
 XCH = T // XW
-GS = 512
-NS = E * C // GS
+SLICES = ((0, 256), (256, 256), (512, 512), (1024, 512), (1536, 512))
+NS = len(SLICES)
+TOKENS_AT = {0: (1, 2), 2: (3,), 4: (4,)}
 HALF = 128
 NB = N // P
 GA = 512
@@ -85,22 +86,24 @@ def tile_routed_moe_kernel(tc, xT, w1, w2, gate, offs, out):
                 else:
                     nc.scalar.copy(out=dst, in_=src)
 
-        xg = [keep.tile([P, GS, 4], BF16, name="xg%d" % s, align_bytes=64) for s in range(NS)]
+        xg = [keep.tile([P, n, 4], BF16, name="xg%d" % s, align_bytes=64) for s, (lo, n) in enumerate(SLICES)]
         xq_pool = ctx.enter_context(tc.tile_pool(name="xq_pool", bufs=1))
         xc = {}
         xs = {}
 
         def gather(u, s):
+            lo, n = SLICES[s]
             window = pairs[:, u, :, :].rearrange("p n e -> p (n e)").bitcast(U32)
             words = xg[s][:].rearrange("p n t -> p (n t)").bitcast(U32).rearrange("p (n u) -> p n u", u=2)
             nc.vector.tensor_copy(
                 out=words[:, :, u],
-                in_=window.indirect(offsets[:, s * GS // 16 : (s + 1) * GS // 16]),
+                in_=window.indirect(offsets[:, lo // 16 : (lo + n) // 16]),
             )
 
         def quantize_tokens(s):
-            xc[s] = xq_pool.tile([P, GS], U32, name="xc", align_bytes=64)
-            xs[s] = xq_pool.tile([P, GS], U8, name="xs", align_bytes=64)
+            n = SLICES[s][1]
+            xc[s] = xq_pool.tile([P, n], U32, name="xc", align_bytes=64)
+            xs[s] = xq_pool.tile([P, n], U8, name="xs", align_bytes=64)
             nc.vector.quantize_mx(
                 out=xc[s][:].bitcast(FP8X4),
                 scales=xs[s][:],
@@ -109,8 +112,8 @@ def tile_routed_moe_kernel(tc, xT, w1, w2, gate, offs, out):
 
         wq = {}
 
-        def prepare_weights(e):
-            for layer in (1, 2):
+        def prepare_weights(e, layers=(1, 2)):
+            for layer in layers:
                 raw = wraw[(layer, e)]
                 grouped = wg_pool.tile([P, 4 * 512], BF16, name="grouped", align_bytes=64)
                 if layer == 1:
@@ -135,7 +138,8 @@ def tile_routed_moe_kernel(tc, xT, w1, w2, gate, offs, out):
         hq = {}
 
         def first_layer(e):
-            s, col = (e * C) // GS, (e * C) % GS
+            s = [i for i, (lo, n) in enumerate(SLICES) if lo <= e * C < lo + n][0]
+            col = e * C - SLICES[s][0]
             c1, s1 = wq[(1, e)]
             hg = h_pool.tile([P, C, 4], BF16, name="hg", align_bytes=64)
             for half in range(C // HALF):
@@ -181,7 +185,17 @@ def tile_routed_moe_kernel(tc, xT, w1, w2, gate, offs, out):
             y = y_pool.tile([P, NB, C], F32, name="y")
             for q in range(NB // 2):
                 second_layer_bank([(e, 2 * q), (e, 2 * q + 1)], y[:, 2 * q : 2 * q + 2, :])
-            staged[e] = y
+            staged[e] = [y[:, nb, :] for nb in range(NB)]
+
+        def second_layer_of_first_expert():
+            y = y_pool.tile([P, NB, C], F32, name="y")
+            second_layer_bank([(0, 0), (0, 1)], y[:, 0:2, :])
+            load_weights(2)
+            prepare_weights(2, (1,))
+            late = wraw[(1, 2)][:, 0, :].rearrange("p (a c) -> p a c", a=2)
+            second_layer_bank([(0, 2), (0, 3)], late)
+            prepare_weights(2, (2,))
+            staged[0] = [y[:, 0, :], y[:, 1, :], late[:, 0, :], late[:, 1, :]]
 
         def scatter(nb, sums, e, n_experts):
             lo, hi = e * C, (e + n_experts) * C
@@ -193,7 +207,7 @@ def tile_routed_moe_kernel(tc, xT, w1, w2, gate, offs, out):
 
         def way_back(e):
             for nb in range(NB):
-                scatter(nb, staged[e][:, nb, :], e, 1)
+                scatter(nb, staged[e][nb], e, 1)
 
         def last_two_experts():
             a, b = E - 2, E - 1
@@ -222,13 +236,16 @@ def tile_routed_moe_kernel(tc, xT, w1, w2, gate, offs, out):
         prepare_weights(1)
         first_layer(0)
         for e in range(E - 2):
-            if e % 2 == 0 and e // 2 + 1 < NS:
-                gather(1, e // 2 + 1)
-                quantize_tokens(e // 2 + 1)
+            for s in TOKENS_AT.get(e, ()):
+                gather(1, s)
+                quantize_tokens(s)
             first_layer(e + 1)
-            second_layer(e)
-            load_weights(e + 2)
-            prepare_weights(e + 2)
+            if e == 0:
+                second_layer_of_first_expert()
+            else:
+                second_layer(e)
+                load_weights(e + 2)
+                prepare_weights(e + 2)
             way_back(e)
         first_layer(E - 1)
         last_two_experts()

@@ -54,13 +54,20 @@ def tile_routed_moe_kernel(tc, xT, w1, w2, gate, offs, out):
             nc.sync.dma_start(out=xraw[(u, c)][:], in_=x_view[:, 2 * u : 2 * u + 2, c * XW : (c + 1) * XW])
 
         wraw = {}
+        lent_to_h = {}
 
         def load_weight(layer, e):
             if (layer, e) in wraw:
                 return
             w = w1 if layer == 1 else w2
-            wraw[(layer, e)] = wraw_pool.tile([P, 4, 512], F32, name="wraw")
-            nc.sync.dma_start(out=wraw[(layer, e)][:], in_=w[e, :, :].rearrange("(p j) c -> p j c", j=4))
+            if (layer, e) == (1, 1):
+                lent = wraw_pool.tile([P, 2 * 4 * 512], BF16, name="wraw", align_bytes=64)
+                lent_to_h[0] = lent
+                wraw[(layer, e)] = lent[:].bitcast(F32).rearrange("p (j c) -> p j c", j=4)
+            else:
+                plain = wraw_pool.tile([P, 4, 512], F32, name="wraw", align_bytes=64)
+                wraw[(layer, e)] = plain[:]
+            nc.sync.dma_start(out=wraw[(layer, e)], in_=w[e, :, :].rearrange("(p j) c -> p j c", j=4))
 
         def load_weights(e):
             load_weight(1, e)
@@ -87,7 +94,7 @@ def tile_routed_moe_kernel(tc, xT, w1, w2, gate, offs, out):
                     nc.scalar.copy(out=dst, in_=src)
 
         xg = [keep.tile([P, n, 4], BF16, name="xg%d" % s, align_bytes=64) for s, (lo, n) in enumerate(SLICES)]
-        xq_pool = ctx.enter_context(tc.tile_pool(name="xq_pool", bufs=1))
+        xq_pool = ctx.enter_context(tc.tile_pool(name="xq_pool", bufs=2))
         xc = {}
         xs = {}
 
@@ -118,10 +125,10 @@ def tile_routed_moe_kernel(tc, xT, w1, w2, gate, offs, out):
                 grouped = wg_pool.tile([P, 4 * 512], BF16, name="grouped", align_bytes=64)
                 if layer == 1:
                     dst = grouped[:].rearrange("p (t m j) -> p m j t", t=4, j=4)
-                    src = raw[:].rearrange("p j (m t) -> p m j t", t=4)
+                    src = raw.rearrange("p j (m t) -> p m j t", t=4)
                 else:
                     dst = grouped[:].rearrange("p (c i j) -> p c j i", i=4, j=4)
-                    src = raw[:].rearrange("p j (c i) -> p c j i", i=4)
+                    src = raw.rearrange("p j (c i) -> p c j i", i=4)
                 if (layer, e) in V_IL:
                     nc.vector.tensor_copy(out=dst, in_=src)
                 elif (layer, e) in G_IL:
@@ -141,7 +148,11 @@ def tile_routed_moe_kernel(tc, xT, w1, w2, gate, offs, out):
             s = [i for i, (lo, n) in enumerate(SLICES) if lo <= e * C < lo + n][0]
             col = e * C - SLICES[s][0]
             c1, s1 = wq[(1, e)]
-            hg = h_pool.tile([P, C, 4], BF16, name="hg", align_bytes=64)
+            if e == 0:
+                hg = lent_to_h[0][:, 0 : 4 * C].rearrange("p (n t) -> p n t", t=4)
+            else:
+                own = h_pool.tile([P, C, 4], BF16, name="hg", align_bytes=64)
+                hg = own[:]
             for half in range(C // HALF):
                 lo = col + half * HALF
                 ps1 = ps_pool.tile([P, 4, HALF], F32, name="bank")
@@ -162,7 +173,7 @@ def tile_routed_moe_kernel(tc, xT, w1, w2, gate, offs, out):
                 )
             hc = h_pool.tile([P, C], U32, name="hc", align_bytes=64)
             hs = h_pool.tile([P, C], U8, name="hs", align_bytes=64)
-            nc.vector.quantize_mx(out=hc[:].bitcast(FP8X4), scales=hs[:], in_=hg[:].rearrange("p n t -> p (n t)"))
+            nc.vector.quantize_mx(out=hc[:].bitcast(FP8X4), scales=hs[:], in_=hg.rearrange("p n t -> p (n t)"))
             hq[e] = (hc, hs)
 
         def second_layer_bank(blocks, dst):

@@ -20,6 +20,7 @@ XCH = T // XW
 SLICES = ((0, 256), (256, 256), (512, 512), (1024, 512), (1536, 512))
 NS = len(SLICES)
 TOKENS_AT = {0: (1, 2), 2: (3,), 4: (4,)}
+HELD_BACK = (3, 4)
 HALF = 128
 NB = N // P
 GA = 512
@@ -118,11 +119,13 @@ def tile_routed_moe_kernel(tc, xT, w1, w2, gate, offs, out):
             )
 
         wq = {}
+        wgrouped = {}
 
         def prepare_weights(e, layers=(1, 2)):
             for layer in layers:
                 raw = wraw[(layer, e)]
                 grouped = wg_pool.tile([P, 4 * 512], BF16, name="grouped", align_bytes=64)
+                wgrouped[(layer, e)] = grouped
                 if layer == 1:
                     dst = grouped[:].rearrange("p (t m j) -> p m j t", t=4, j=4)
                     src = raw.rearrange("p j (m t) -> p m j t", t=4)
@@ -245,6 +248,8 @@ def tile_routed_moe_kernel(tc, xT, w1, w2, gate, offs, out):
         quantize_tokens(0)
         prepare_weights(0)
         prepare_weights(1)
+        for s in HELD_BACK:
+            nc.vector.tensor_copy(out=xg[s][:, 0, 2:4], in_=wgrouped[(1, 1)][:, 0:2])
         first_layer(0)
         for e in range(E - 2):
             for s in TOKENS_AT.get(e, ()):

@@ -20,7 +20,7 @@ XCH = T // XW
 SLICES = ((0, 256), (256, 256), (512, 512), (1024, 512), (1536, 512))
 NS = len(SLICES)
 TOKENS_AT = {0: (1, 2), 2: (3,), 4: (4,)}
-HELD_BACK = (3, 4)
+HELD_BACK = (4,)
 HALF = 128
 NB = N // P
 GA = 512

@@ -14,18 +14,22 @@ FP8X4 = mybir.dt.float8_e4m3fn_x4
 SILU = mybir.ActivationFunctionType.Silu
 MULT = mybir.AluOpType.mult
 
+NUMS = tuple(str(v) for v in range(-1, 64))
 P = 128
 XW = 512
-XCH = T // XW
 SLICES = ((0, 256), (256, 256), (512, 512), (1024, 512), (1536, 512))
-NS = len(SLICES)
-TOKENS_AT = {0: (1, 2), 2: (3,), 4: (4,)}
-HELD_BACK = (4,)
 HALF = 128
 NB = N // P
-GA = 512
-V_IL = ((2, 1),)
-G_IL = ()
+STEPS = """
+lx,0,0 lx,0,1 lx,0,2 lx,0,3 lx,1,0 lx,1,1 lx,1,2 lx,1,3 lw,1,0 lw,2,0 lw,1,1,lent lg,0,8 lw,2,1 r,0,0,V r,0,1,V r,0,2,V r,0,3,V
+r,1,0,S r,1,1,S r,1,2,S r,1,3,S g,0,0 g,0,1 g,0,2 g,0,3 g,0,4 g,1,0 q,0 i,1,0,S k,1,0 i,2,0,S k,2,0 i,1,1,S k,1,1 i,2,1,V k,2,1
+pin,4,1,1 f,0,0 f,0,1 h,0 g,1,1 q,1 g,1,2 q,2 f,1,0 f,1,1 h,1 s,0,0 lw,1,2 lw,2,2 i,1,2,S k,1,2 s,0,1,1,2,0 i,2,2,S k,2,2 t,0,0
+t,0,1 t,0,2 t,0,3 f,2,0 f,2,1 h,2 s,1,0 s,1,1 lw,1,3 lw,2,3 i,1,3,S k,1,3 i,2,3,S k,2,3 t,1,0 t,1,1 t,1,2 t,1,3 g,1,3 q,3 f,3,0
+f,3,1 h,3 s,2,0 s,2,1 lw,1,4 lw,2,4 i,1,4,S k,1,4 i,2,4,S k,2,4 t,2,0 t,2,1 t,2,2 t,2,3 f,4,0 f,4,1 h,4 s,3,0 s,3,1 lw,1,5 lw,2,5
+i,1,5,S k,1,5 i,2,5,S k,2,5 t,3,0 t,3,1 t,3,2 t,3,3 g,1,4 q,4 f,5,0 f,5,1 h,5 s,4,0 s,4,1 lw,1,6 lw,2,6 i,1,6,S k,1,6 i,2,6,S
+k,2,6 t,4,0 t,4,1 t,4,2 t,4,3 f,6,0 f,6,1 h,6 s,5,0 s,5,1 lw,1,7 lw,2,7 i,1,7,S k,1,7 i,2,7,S k,2,7 t,5,0 t,5,1 t,5,2 t,5,3 f,7,0
+f,7,1 h,7 s,6,0 s,7,0 m,2 m,3 t,6,0 t,6,1 t,7,0 o,0 t,7,1 o,1 t,-1,2 o,2 t,-1,3 o,3
+"""
 
 
 def tile_routed_moe_kernel(tc, xT, w1, w2, gate, offs, out):
@@ -37,231 +41,201 @@ def tile_routed_moe_kernel(tc, xT, w1, w2, gate, offs, out):
         wq_pool = ctx.enter_context(tc.tile_pool(name="wq_pool", bufs=3))
         h_pool = ctx.enter_context(tc.tile_pool(name="h_pool", bufs=3))
         y_pool = ctx.enter_context(tc.tile_pool(name="y_pool", bufs=3))
+        xq_pool = ctx.enter_context(tc.tile_pool(name="xq_pool", bufs=5))
         ps_pool = ctx.enter_context(tc.psum_pool(name="ps_pool", bufs=2))
 
         offsets = keep.tile([P, E * C // 16], U16, name="offsets")
         nc.sync.dma_start(offsets[:], offs)
-
         warm_in = keep.tile([P, 1], F32, name="warm_in")
         warm_out = keep.tile([P, 1], F32, name="warm_out")
         nc.gpsimd.memset(warm_in[:], 0.0)
         nc.scalar.activation(out=warm_out[:], in_=warm_in[:], func=SILU)
 
         x_view = xT.rearrange("(p t) n -> p t n", t=4)
-        xraw = {}
-
-        def load_x(u, c):
-            xraw[(u, c)] = keep.tile([P, 2, XW], F32, name="xraw%d_%d" % (u, c))
-            nc.sync.dma_start(out=xraw[(u, c)][:], in_=x_view[:, 2 * u : 2 * u + 2, c * XW : (c + 1) * XW])
-
-        wraw = {}
-        lent_to_h = {}
-
-        def load_weight(layer, e):
-            if (layer, e) in wraw:
-                return
-            w = w1 if layer == 1 else w2
-            if (layer, e) == (1, 1):
-                lent = wraw_pool.tile([P, 2 * 4 * 512], BF16, name="wraw", align_bytes=64)
-                lent_to_h[0] = lent
-                wraw[(layer, e)] = lent[:].bitcast(F32).rearrange("p (j c) -> p j c", j=4)
-            else:
-                plain = wraw_pool.tile([P, 4, 512], F32, name="wraw", align_bytes=64)
-                wraw[(layer, e)] = plain[:]
-            nc.sync.dma_start(out=wraw[(layer, e)], in_=w[e, :, :].rearrange("(p j) c -> p j c", j=4))
-
-        def load_weights(e):
-            load_weight(1, e)
-            load_weight(2, e)
-
         gate_sb = keep.tile([P, E * C], F32, name="gate_sb")
-        load_weight(1, 0)
-        for u in range(2):
-            for c in range(XCH):
-                load_x(u, c)
-        load_weight(2, 0)
-        load_weight(1, 1)
-        nc.sync.dma_start(out=gate_sb[:], in_=gate[0:P, :])
-        load_weight(2, 1)
-
         pairs = keep.tile([P, 2, T, 2], BF16, name="pairs")
-        for u in range(2):
-            for c in range(XCH):
-                dst = pairs[:, u, c * XW : (c + 1) * XW, :]
-                src = xraw[(u, c)][:].rearrange("p e n -> p n e")
-                if u == 0:
-                    nc.vector.tensor_copy(out=dst, in_=src)
-                else:
-                    nc.scalar.copy(out=dst, in_=src)
-
+        out_sb = [keep.tile([P, T], F32, name="out_sb%d" % nb) for nb in range(NB)]
         xg = [keep.tile([P, n, 4], BF16, name="xg%d" % s, align_bytes=64) for s, (lo, n) in enumerate(SLICES)]
-        xq_pool = ctx.enter_context(tc.tile_pool(name="xq_pool", bufs=2))
-        xc = {}
-        xs = {}
-
-        def gather(u, s):
-            lo, n = SLICES[s]
-            window = pairs[:, u, :, :].rearrange("p n e -> p (n e)").bitcast(U32)
-            words = xg[s][:].rearrange("p n t -> p (n t)").bitcast(U32).rearrange("p (n u) -> p n u", u=2)
-            nc.vector.tensor_copy(
-                out=words[:, :, u],
-                in_=window.indirect(offsets[:, lo // 16 : (lo + n) // 16]),
-            )
-
-        def quantize_tokens(s):
-            n = SLICES[s][1]
-            xc[s] = xq_pool.tile([P, n], U32, name="xc", align_bytes=64)
-            xs[s] = xq_pool.tile([P, n], U8, name="xs", align_bytes=64)
-            nc.vector.quantize_mx(
-                out=xc[s][:].bitcast(FP8X4),
-                scales=xs[s][:],
-                in_=xg[s][:].rearrange("p n t -> p (n t)"),
-            )
-
+        xraw = {}
+        wraw = {}
+        grp = {}
         wq = {}
-        wgrouped = {}
+        xq = {}
+        hg = {}
+        hq = {}
+        y = {}
+        stg = {}
+        stamp = keep.tile([P, 8], U32, name="stamp")
+        n_stamp = 0
 
-        def prepare_weights(e, layers=(1, 2)):
-            for layer in layers:
+        def cast(eng, dst, src):
+            if eng == "V":
+                nc.vector.tensor_copy(out=dst, in_=src)
+            elif eng == "S":
+                nc.scalar.copy(out=dst, in_=src)
+            else:
+                nc.gpsimd.tensor_scalar(dst, src, 1.0, 0.0, MULT, mybir.AluOpType.add)
+
+        def y_plane(e, b):
+            if e not in y:
+                tile_y = y_pool.tile([P, NB, C], F32, name="y")
+                y[e] = tile_y
+            return y[e][:, 2 * b : 2 * b + 2, :]
+
+        for step in STEPS.split():
+            op = step.split(",")
+            k = op[0]
+            a = [int(v) if v.replace("-", "") in NUMS else v for v in op[1:]]
+            if k == "lx":
+                u, c = a[0], a[1]
+                n = a[2] if len(a) > 2 else 1
+                t_x = keep.tile([P, 2, n * XW], F32, name="xraw%d_%d" % (u, c))
+                nc.sync.dma_start(out=t_x[:], in_=x_view[:, 2 * u : 2 * u + 2, c * XW : (c + n) * XW])
+                for i in range(n):
+                    xraw[(u, c + i)] = t_x[:, :, i * XW : (i + 1) * XW]
+            elif k == "lw":
+                layer, e = a[0], a[1]
+                w = w1 if layer == 1 else w2
+                if len(a) > 2:
+                    t_b = wraw_pool.tile([P, 2 * 4 * 512], BF16, name="wraw", align_bytes=64)
+                    hg[0] = t_b[:, 0 : 4 * C].rearrange("p (n t) -> p n t", t=4)
+                    wraw[(layer, e)] = t_b[:].bitcast(F32).rearrange("p (j c) -> p j c", j=4)
+                else:
+                    t_w = wraw_pool.tile([P, 4, 512], F32, name="wraw", align_bytes=64)
+                    wraw[(layer, e)] = t_w[:]
+                nc.sync.dma_start(out=wraw[(layer, e)], in_=w[e, :, :].rearrange("(p j) c -> p j c", j=4))
+            elif k == "lg":
+                lo, hi = a[0] * C, a[1] * C
+                nc.sync.dma_start(out=gate_sb[:, lo:hi], in_=gate[0:P, lo:hi])
+            elif k == "r":
+                u, c, eng = a[0], a[1], a[2]
+                lo, hi = (a[3] * 128, a[4] * 128) if len(a) > 3 else (0, XW)
+                cast(eng, pairs[:, u, c * XW + lo : c * XW + hi, :], xraw[(u, c)][:, :, lo:hi].rearrange("p e n -> p n e"))
+            elif k == "g":
+                u, s = a
+                lo, n = SLICES[s]
+                window = pairs[:, u, :, :].rearrange("p n e -> p (n e)").bitcast(U32)
+                words = xg[s][:].rearrange("p n t -> p (n t)").bitcast(U32).rearrange("p (n u) -> p n u", u=2)
+                nc.vector.tensor_copy(out=words[:, :, u], in_=window.indirect(offsets[:, lo // 16 : (lo + n) // 16]))
+            elif k == "q":
+                s = a[0]
+                n = SLICES[s][1]
+                xc = xq_pool.tile([P, n], U32, name="xc", align_bytes=64)
+                xs = xq_pool.tile([P, n], U8, name="xs", align_bytes=64)
+                xq[s] = (xc, xs)
+                nc.vector.quantize_mx(out=xc[:].bitcast(FP8X4), scales=xs[:], in_=xg[s][:].rearrange("p n t -> p (n t)"))
+            elif k == "i":
+                layer, e, eng = a[0], a[1], a[2]
+                parts = a[3] if len(a) > 3 else 1
+                t_g = wg_pool.tile([P, 4 * 512], BF16, name="grouped", align_bytes=64)
+                grp[(layer, e)] = t_g
                 raw = wraw[(layer, e)]
-                grouped = wg_pool.tile([P, 4 * 512], BF16, name="grouped", align_bytes=64)
-                wgrouped[(layer, e)] = grouped
-                if layer == 1:
-                    dst = grouped[:].rearrange("p (t m j) -> p m j t", t=4, j=4)
-                    src = raw.rearrange("p j (m t) -> p m j t", t=4)
-                else:
-                    dst = grouped[:].rearrange("p (c i j) -> p c j i", i=4, j=4)
-                    src = raw.rearrange("p j (c i) -> p c j i", i=4)
-                if (layer, e) in V_IL:
-                    nc.vector.tensor_copy(out=dst, in_=src)
-                elif (layer, e) in G_IL:
-                    nc.gpsimd.tensor_scalar(dst, src, 1.0, 0.0, MULT, mybir.AluOpType.add)
-                else:
-                    nc.scalar.copy(out=dst, in_=src)
+                for part in range(parts):
+                    if eng == "G":
+                        w = 512 // parts
+                        if layer == 2:
+                            dst = t_g[:, 4 * w * part : 4 * w * (part + 1)].rearrange("p (c j) -> p c j", j=4)
+                            src = raw[:, :, w * part : w * (part + 1)].rearrange("p j c -> p c j")
+                        else:
+                            mm = 128 // parts
+                            dst = t_g[:].rearrange("p (t m j) -> p t m j", t=4, j=4)[:, :, mm * part : mm * (part + 1), :]
+                            src = raw.rearrange("p j (m t) -> p t m j", t=4)[:, :, mm * part : mm * (part + 1), :]
+                    elif layer == 1:
+                        dst = t_g[:].rearrange("p (t m j) -> p m j t", t=4, j=4)
+                        src = raw.rearrange("p j (m t) -> p m j t", t=4)
+                    else:
+                        dst = t_g[:].rearrange("p (c i j) -> p c j i", i=4, j=4)
+                        src = raw.rearrange("p j (c i) -> p c j i", i=4)
+                    cast(eng, dst, src)
+            elif k == "k":
+                layer, e = a
                 codes = wq_pool.tile([P, 512], U32, name="codes%d" % layer, align_bytes=64)
                 scales = wq_pool.tile([P, 512], U8, name="scales%d" % layer, align_bytes=64)
-                nc.vector.quantize_mx(out=codes[:].bitcast(FP8X4), scales=scales[:], in_=grouped[:])
                 wq[(layer, e)] = (codes, scales)
-
-        out_sb = [keep.tile([P, T], F32, name="out_sb%d" % nb) for nb in range(NB)]
-        staged = {}
-        hq = {}
-
-        def first_layer(e):
-            s = [i for i, (lo, n) in enumerate(SLICES) if lo <= e * C < lo + n][0]
-            col = e * C - SLICES[s][0]
-            c1, s1 = wq[(1, e)]
-            if e == 0:
-                hg = lent_to_h[0][:, 0 : 4 * C].rearrange("p (n t) -> p n t", t=4)
-            else:
-                own = h_pool.tile([P, C, 4], BF16, name="hg", align_bytes=64)
-                hg = own[:]
-            for half in range(C // HALF):
-                lo = col + half * HALF
+                nc.vector.quantize_mx(out=codes[:].bitcast(FP8X4), scales=scales[:], in_=grp[(layer, e)][:])
+            elif k == "pin":
+                s, layer, e = a
+                nc.vector.tensor_copy(out=xg[s][:, 0, 2:4], in_=grp[(layer, e)][:, 0:2])
+            elif k == "pin0":
+                s, layer, e = a
+                nc.vector.tensor_copy(out=xg[s][:, 0, 0:2], in_=grp[(layer, e)][:, 0:2])
+            elif k == "f":
+                e, half = a
+                s = [i for i, (lo, n) in enumerate(SLICES) if lo <= e * C < lo + n][0]
+                lo = e * C - SLICES[s][0] + half * HALF
+                c1, s1 = wq[(1, e)]
+                xc, xs = xq[s]
+                if e not in hg:
+                    t_h = h_pool.tile([P, C, 4], BF16, name="hg", align_bytes=64)
+                    hg[e] = t_h[:]
                 ps1 = ps_pool.tile([P, 4, HALF], F32, name="bank")
                 for t in range(4):
                     nc.tensor.matmul_mx(
                         out=ps1[:, t, :],
                         lhsT=c1[:, t * P : (t + 1) * P].bitcast(FP8X4),
                         lhsT_scale=s1[:, t * P : (t + 1) * P],
-                        rhs=xc[s][:, lo : lo + HALF].bitcast(FP8X4),
-                        rhs_scale=xs[s][:, lo : lo + HALF],
+                        rhs=xc[:, lo : lo + HALF].bitcast(FP8X4),
+                        rhs_scale=xs[:, lo : lo + HALF],
                         start=True,
                         stop=True,
                     )
-                nc.scalar.activation(
-                    out=hg[:, half * HALF : (half + 1) * HALF, :],
-                    in_=ps1[:].rearrange("p t n -> p n t"),
-                    func=SILU,
-                )
-            hc = h_pool.tile([P, C], U32, name="hc", align_bytes=64)
-            hs = h_pool.tile([P, C], U8, name="hs", align_bytes=64)
-            nc.vector.quantize_mx(out=hc[:].bitcast(FP8X4), scales=hs[:], in_=hg.rearrange("p n t -> p (n t)"))
-            hq[e] = (hc, hs)
-
-        def second_layer_bank(blocks, dst):
-            ps2 = ps_pool.tile([P, 2, C], F32, name="bank")
-            for i, (e, nb) in enumerate(blocks):
-                c2, s2 = wq[(2, e)]
-                hc, hs = hq[e]
-                nc.tensor.matmul_mx(
-                    out=ps2[:, i, :],
-                    lhsT=c2[:, nb * P : (nb + 1) * P].bitcast(FP8X4),
-                    lhsT_scale=s2[:, nb * P : (nb + 1) * P],
-                    rhs=hc[:].bitcast(FP8X4),
-                    rhs_scale=hs[:],
-                    start=True,
-                    stop=True,
-                )
-            nc.scalar.copy(out=dst, in_=ps2[:])
-
-        def second_layer(e):
-            y = y_pool.tile([P, NB, C], F32, name="y")
-            for q in range(NB // 2):
-                second_layer_bank([(e, 2 * q), (e, 2 * q + 1)], y[:, 2 * q : 2 * q + 2, :])
-            staged[e] = [y[:, nb, :] for nb in range(NB)]
-
-        def second_layer_of_first_expert():
-            y = y_pool.tile([P, NB, C], F32, name="y")
-            second_layer_bank([(0, 0), (0, 1)], y[:, 0:2, :])
-            load_weights(2)
-            prepare_weights(2, (1,))
-            late = wraw[(1, 2)][:, 0, :].rearrange("p (a c) -> p a c", a=2)
-            second_layer_bank([(0, 2), (0, 3)], late)
-            prepare_weights(2, (2,))
-            staged[0] = [y[:, 0, :], y[:, 1, :], late[:, 0, :], late[:, 1, :]]
-
-        def scatter(nb, sums, e, n_experts):
-            lo, hi = e * C, (e + n_experts) * C
-            window = out_sb[nb][:].indirect(offsets[:, lo // 16 : hi // 16])
-            nc.vector.tensor_tensor(window, sums, gate_sb[:, lo:hi], MULT)
-
-        def store(nb):
-            nc.sync.dma_start(out=out[nb * P : (nb + 1) * P, :], in_=out_sb[nb][:])
-
-        def way_back(e):
-            for nb in range(NB):
-                scatter(nb, staged[e][nb], e, 1)
-
-        def last_two_experts():
-            a, b = E - 2, E - 1
-            ya = y_pool.tile([P, NB, C], F32, name="y")
-            yb = y_pool.tile([P, NB, C], F32, name="y")
-            second_layer_bank([(a, 0), (a, 1)], ya[:, 0:2, :])
-            second_layer_bank([(b, 0), (b, 1)], yb[:, 0:2, :])
-            second_layer_bank([(a, 2), (b, 2)], ya[:, 2:4, :])
-            second_layer_bank([(a, 3), (b, 3)], yb[:, 2:4, :])
-            scatter(0, ya[:, 0, :], a, 1)
-            scatter(1, ya[:, 1, :], a, 1)
-            scatter(0, yb[:, 0, :], b, 1)
-            store(0)
-            scatter(1, yb[:, 1, :], b, 1)
-            store(1)
-            scatter(2, ya[:, 2:4, :].rearrange("p a c -> p (a c)"), a, 2)
-            store(2)
-            scatter(3, yb[:, 2:4, :].rearrange("p a c -> p (a c)"), a, 2)
-            store(3)
-
-        for s in range(NS):
-            gather(0, s)
-        gather(1, 0)
-        quantize_tokens(0)
-        prepare_weights(0)
-        prepare_weights(1)
-        for s in HELD_BACK:
-            nc.vector.tensor_copy(out=xg[s][:, 0, 2:4], in_=wgrouped[(1, 1)][:, 0:2])
-        first_layer(0)
-        for e in range(E - 2):
-            for s in TOKENS_AT.get(e, ()):
-                gather(1, s)
-                quantize_tokens(s)
-            first_layer(e + 1)
-            if e == 0:
-                second_layer_of_first_expert()
-            else:
-                second_layer(e)
-                load_weights(e + 2)
-                prepare_weights(e + 2)
-            way_back(e)
-        first_layer(E - 1)
-        last_two_experts()
+                nc.scalar.activation(out=hg[e][:, half * HALF : (half + 1) * HALF, :], in_=ps1[:].rearrange("p t n -> p n t"), func=SILU)
+            elif k == "h":
+                e = a[0]
+                hc = h_pool.tile([P, C], U32, name="hc", align_bytes=64)
+                hs = h_pool.tile([P, C], U8, name="hs", align_bytes=64)
+                hq[e] = (hc, hs)
+                nc.vector.quantize_mx(out=hc[:].bitcast(FP8X4), scales=hs[:], in_=hg[e].rearrange("p n t -> p (n t)"))
+            elif k == "s" or k == "m":
+                if k == "s":
+                    e, b = a[0], a[1]
+                    blocks = ((e, 2 * b), (e, 2 * b + 1))
+                    if len(a) > 2:
+                        plane = wraw[(a[2], a[3])][:, a[4], :].rearrange("p (a c) -> p a c", a=2)
+                    else:
+                        plane = y_plane(e, b)
+                    stg[(e, 2 * b)] = plane[:, 0, :]
+                    stg[(e, 2 * b + 1)] = plane[:, 1, :]
+                else:
+                    nb = a[0]
+                    blocks = ((E - 2, nb), (E - 1, nb))
+                    plane = y_plane(E - 4 + nb, 1)
+                    stg[(-1, nb)] = plane.rearrange("p a c -> p (a c)")
+                ps2 = ps_pool.tile([P, 2, C], F32, name="bank")
+                for i, (e, nb) in enumerate(blocks):
+                    c2, s2 = wq[(2, e)]
+                    hc, hs = hq[e]
+                    nc.tensor.matmul_mx(
+                        out=ps2[:, i, :],
+                        lhsT=c2[:, nb * P : (nb + 1) * P].bitcast(FP8X4),
+                        lhsT_scale=s2[:, nb * P : (nb + 1) * P],
+                        rhs=hc[:].bitcast(FP8X4),
+                        rhs_scale=hs[:],
+                        start=True,
+                        stop=True,
+                    )
+                nc.scalar.copy(out=plane, in_=ps2[:])
+            elif k == "t":
+                e, nb = a
+                lo, hi = (e * C, (e + 1) * C) if e >= 0 else ((E - 2) * C, E * C)
+                window = out_sb[nb][:].indirect(offsets[:, lo // 16 : hi // 16])
+                nc.vector.tensor_tensor(window, stg[(e, nb)], gate_sb[:, lo:hi], MULT)
+            elif k == "o":
+                nb = a[0]
+                nc.sync.dma_start(out=out[nb * P : (nb + 1) * P, :], in_=out_sb[nb][:])
+            elif k == "z":
+                what = a[0]
+                if what == "h":
+                    probe = hq[a[1]][0][:, 0:1]
+                elif what == "y":
+                    probe = stg[(a[1], a[2])][:, 0:1].bitcast(U32)
+                elif what == "g":
+                    probe = grp[(a[1], a[2])][:, 0:2].bitcast(U32)
+                elif what == "p":
+                    probe = pairs[:, a[1], T - 1, :].bitcast(U32)
+                elif what == "k":
+                    probe = wq[(a[1], a[2])][0][:, 0:1]
+                else:
+                    probe = out_sb[a[1]][:, 0:1].bitcast(U32)
+                nc.gpsimd.tensor_copy(out=stamp[:, n_stamp : n_stamp + 1], in_=probe)
+                n_stamp += 1

@@ -21,14 +21,14 @@ SLICES = ((0, 256), (256, 256), (512, 512), (1024, 512), (1536, 512))
 HALF = 128
 NB = N // P
 STEPS = """
-lx,0,0 lx,0,1 lx,0,2 lx,0,3 lx,1,0 lx,1,1 lx,1,2 lx,1,3 lw,1,0 lw,2,0 lw,1,1,lent lg,0,8 lw,2,1 r,0,0,V r,0,1,V r,0,2,V r,0,3,V
-r,1,0,S r,1,1,S r,1,2,S r,1,3,S g,0,0 g,0,1 g,0,2 g,0,3 g,0,4 g,1,0 q,0 i,1,0,S k,1,0 i,2,0,S k,2,0 i,1,1,S k,1,1 i,2,1,V k,2,1
-pin,4,1,1 f,0,0 f,0,1 h,0 g,1,1 q,1 g,1,2 q,2 f,1,0 f,1,1 h,1 s,0,0 lw,1,2 lw,2,2 i,1,2,S k,1,2 s,0,1,1,2,0 i,2,2,S k,2,2 t,0,0
-t,0,1 t,0,2 t,0,3 f,2,0 f,2,1 h,2 s,1,0 s,1,1 lw,1,3 lw,2,3 i,1,3,S k,1,3 i,2,3,S k,2,3 t,1,0 t,1,1 t,1,2 t,1,3 g,1,3 q,3 f,3,0
-f,3,1 h,3 s,2,0 s,2,1 lw,1,4 lw,2,4 i,1,4,S k,1,4 i,2,4,S k,2,4 t,2,0 t,2,1 t,2,2 t,2,3 f,4,0 f,4,1 h,4 s,3,0 s,3,1 lw,1,5 lw,2,5
-i,1,5,S k,1,5 i,2,5,S k,2,5 t,3,0 t,3,1 t,3,2 t,3,3 g,1,4 q,4 f,5,0 f,5,1 h,5 s,4,0 s,4,1 lw,1,6 lw,2,6 i,1,6,S k,1,6 i,2,6,S
-k,2,6 t,4,0 t,4,1 t,4,2 t,4,3 f,6,0 f,6,1 h,6 s,5,0 s,5,1 lw,1,7 lw,2,7 i,1,7,S k,1,7 i,2,7,S k,2,7 t,5,0 t,5,1 t,5,2 t,5,3 f,7,0
-f,7,1 h,7 s,6,0 s,7,0 m,2 m,3 t,6,0 t,6,1 t,7,0 o,0 t,7,1 o,1 t,-1,2 o,2 t,-1,3 o,3
+lx,0,0,2 lx,0,2 lx,0,3 of lx,1,0,2 lx,1,2 lx,1,3 lw,1,0 lw,2,0 lw,1,1,lent lg,0,8 lw,2,1 r,0,0,V r,0,1,V r,0,2,V r,0,3,V r,1,0,S
+r,1,1,S r,1,2,S r,1,3,S g,0,0 g,0,1 g,0,2 g,0,3 g,0,4 g,1,0 q,0 i,1,0,S k,1,0 i,2,0,S k,2,0 i,1,1,S k,1,1 i,2,1,V k,2,1 pin,4,1,1
+f,0,0 f,0,1 h,0 g,1,1 q,1 g,1,2 q,2 f,1,0 f,1,1 h,1 s,0,0 lw,1,2 lw,2,2 i,1,2,S k,1,2 s,0,1,1,2,0 i,2,2,S k,2,2 t,0,0 t,0,1 t,0,2
+t,0,3 f,2,0 f,2,1 h,2 s,1,0 s,1,1 lw,1,3 lw,2,3 i,1,3,S k,1,3 i,2,3,S k,2,3 t,1,0 t,1,1 t,1,2 t,1,3 g,1,3 q,3 f,3,0 f,3,1 h,3
+s,2,0 s,2,1 lw,1,4 lw,2,4 i,1,4,S k,1,4 i,2,4,S k,2,4 t,2,0 t,2,1 t,2,2 t,2,3 f,4,0 f,4,1 h,4 s,3,0 s,3,1 lw,1,5 lw,2,5 i,1,5,S
+k,1,5 i,2,5,S k,2,5 t,3,0 t,3,1 t,3,2 t,3,3 g,1,4 q,4 f,5,0 f,5,1 h,5 s,4,0 s,4,1 lw,1,6 lw,2,6 i,1,6,S k,1,6 i,2,6,S k,2,6 t,4,0
+t,4,1 t,4,2 t,4,3 f,6,0 f,6,1 h,6 s,5,0 s,5,1 lw,1,7 lw,2,7 i,1,7,S k,1,7 i,2,7,S k,2,7 t,5,0 t,5,1 t,5,2 t,5,3 f,7,0 f,7,1 h,7
+s,6,0 s,7,0 m,2 m,3 t,6,0 t,6,1 t,7,0 o,0 t,7,1 o,1 t,-1,2 o,2 t,-1,3 o,3
 """
 
 
@@ -45,7 +45,6 @@ def tile_routed_moe_kernel(tc, xT, w1, w2, gate, offs, out):
         ps_pool = ctx.enter_context(tc.psum_pool(name="ps_pool", bufs=2))
 
         offsets = keep.tile([P, E * C // 16], U16, name="offsets")
-        nc.sync.dma_start(offsets[:], offs)
         warm_in = keep.tile([P, 1], F32, name="warm_in")
         warm_out = keep.tile([P, 1], F32, name="warm_out")
         nc.gpsimd.memset(warm_in[:], 0.0)
@@ -57,6 +56,7 @@ def tile_routed_moe_kernel(tc, xT, w1, w2, gate, offs, out):
         out_sb = [keep.tile([P, T], F32, name="out_sb%d" % nb) for nb in range(NB)]
         xg = [keep.tile([P, n, 4], BF16, name="xg%d" % s, align_bytes=64) for s, (lo, n) in enumerate(SLICES)]
         xraw = {}
+        planes = {}
         wraw = {}
         grp = {}
         wq = {}
@@ -86,7 +86,9 @@ def tile_routed_moe_kernel(tc, xT, w1, w2, gate, offs, out):
             op = step.split(",")
             k = op[0]
             a = [int(v) if v.replace("-", "") in NUMS else v for v in op[1:]]
-            if k == "lx":
+            if k == "of":
+                nc.sync.dma_start(offsets[:], offs)
+            elif k == "lx":
                 u, c = a[0], a[1]
                 n = a[2] if len(a) > 2 else 1
                 t_x = keep.tile([P, 2, n * XW], F32, name="xraw%d_%d" % (u, c))
@@ -117,6 +119,23 @@ def tile_routed_moe_kernel(tc, xT, w1, w2, gate, offs, out):
                 window = pairs[:, u, :, :].rearrange("p n e -> p (n e)").bitcast(U32)
                 words = xg[s][:].rearrange("p n t -> p (n t)").bitcast(U32).rearrange("p (n u) -> p n u", u=2)
                 nc.vector.tensor_copy(out=words[:, :, u], in_=window.indirect(offsets[:, lo // 16 : (lo + n) // 16]))
+            elif k == "c":
+                t, c, eng = a
+                if t not in planes:
+                    t_p = keep.tile([P, T], BF16, name="plane%d" % t)
+                    planes[t] = t_p
+                cast(eng, planes[t][:, c * XW : (c + 1) * XW], xraw[(t // 2, c)][:, t % 2, :])
+            elif k == "gs":
+                t, s = a
+                lo, n = SLICES[s]
+                nc.scalar.activation(
+                    out=xg[s][:, :, t],
+                    in_=planes[t][:].indirect(offsets[:, lo // 16 : (lo + n) // 16]),
+                    func=mybir.ActivationFunctionType.Copy,
+                )
+            elif k == "spin":
+                s, layer, e = a
+                nc.scalar.copy(out=xg[s][:, 0, 2:4], in_=grp[(layer, e)][:, 0:2])
             elif k == "q":
                 s = a[0]
                 n = SLICES[s][1]

@@ -22,7 +22,7 @@ HALF = 128
 NB = N // P
 STEPS = """
 lx,0,0,2 lx,0,2 lx,0,3 of lx,1,0,2 lx,1,2 lx,1,3 lw,1,0 lw,2,0 lw,1,1,lent lg,0,8 lw,2,1 r,0,0,V r,0,1,V r,0,2,V r,0,3,V r,1,0,S
-r,1,1,S r,1,2,S r,1,3,S g,0,0 g,0,1 g,0,2 g,0,3 g,0,4 g,1,0 q,0 i,1,0,S k,1,0 i,2,0,S k,2,0 i,1,1,S k,1,1 i,2,1,V k,2,1 pin,4,1,1
+r,1,1,G r,1,2,S r,1,3,S g,0,0 g,0,1 g,0,2 g,0,3 g,0,4 g,1,0 q,0 i,1,0,S k,1,0 i,2,0,S k,2,0 i,1,1,S k,1,1 i,2,1,V k,2,1 pin,4,1,1
 f,0,0 f,0,1 h,0 g,1,1 q,1 g,1,2 q,2 f,1,0 f,1,1 h,1 s,0,0 lw,1,2 lw,2,2 i,1,2,S k,1,2 s,0,1,1,2,0 i,2,2,S k,2,2 t,0,0 t,0,1 t,0,2
 t,0,3 f,2,0 f,2,1 h,2 s,1,0 s,1,1 lw,1,3 lw,2,3 i,1,3,S k,1,3 i,2,3,S k,2,3 t,1,0 t,1,1 t,1,2 t,1,3 g,1,3 q,3 f,3,0 f,3,1 h,3
 s,2,0 s,2,1 lw,1,4 lw,2,4 i,1,4,S k,1,4 i,2,4,S k,2,4 t,2,0 t,2,1 t,2,2 t,2,3 f,4,0 f,4,1 h,4 s,3,0 s,3,1 lw,1,5 lw,2,5 i,1,5,S
@@ -41,6 +41,7 @@ def tile_routed_moe_kernel(tc, xT, w1, w2, gate, offs, out):
         wq_pool = ctx.enter_context(tc.tile_pool(name="wq_pool", bufs=3))
         h_pool = ctx.enter_context(tc.tile_pool(name="h_pool", bufs=3))
         y_pool = ctx.enter_context(tc.tile_pool(name="y_pool", bufs=3))
+        flat_pool = ctx.enter_context(tc.tile_pool(name="flat_pool", bufs=2))
         xq_pool = ctx.enter_context(tc.tile_pool(name="xq_pool", bufs=5))
         ps_pool = ctx.enter_context(tc.psum_pool(name="ps_pool", bufs=2))
 
@@ -57,6 +58,7 @@ def tile_routed_moe_kernel(tc, xT, w1, w2, gate, offs, out):
         xg = [keep.tile([P, n, 4], BF16, name="xg%d" % s, align_bytes=64) for s, (lo, n) in enumerate(SLICES)]
         xraw = {}
         planes = {}
+        flat = {}
         wraw = {}
         grp = {}
         wq = {}
@@ -119,6 +121,20 @@ def tile_routed_moe_kernel(tc, xT, w1, w2, gate, offs, out):
                 window = pairs[:, u, :, :].rearrange("p n e -> p (n e)").bitcast(U32)
                 words = xg[s][:].rearrange("p n t -> p (n t)").bitcast(U32).rearrange("p (n u) -> p n u", u=2)
                 nc.vector.tensor_copy(out=words[:, :, u], in_=window.indirect(offsets[:, lo // 16 : (lo + n) // 16]))
+            elif k == "gc":
+                u, s = a
+                lo, n = SLICES[s]
+                if s not in flat:
+                    t_f = flat_pool.tile([P, 2, n, 2], BF16, name="flat")
+                    flat[s] = t_f
+                window = pairs[:, u, :, :].rearrange("p n e -> p (n e)").bitcast(U32)
+                nc.vector.tensor_copy(
+                    out=flat[s][:, u, :, :].rearrange("p n e -> p (n e)").bitcast(U32),
+                    in_=window.indirect(offsets[:, lo // 16 : (lo + n) // 16]),
+                )
+            elif k == "ic":
+                s, eng = a
+                cast(eng, xg[s][:].rearrange("p n (u e) -> p n u e", u=2), flat[s][:].rearrange("p u n e -> p n u e"))
             elif k == "c":
                 t, c, eng = a
                 if t not in planes:
@@ -133,6 +149,10 @@ def tile_routed_moe_kernel(tc, xT, w1, w2, gate, offs, out):
                     in_=planes[t][:].indirect(offsets[:, lo // 16 : (lo + n) // 16]),
                     func=mybir.ActivationFunctionType.Copy,
                 )
+            elif k == "pg":
+                t_g = wg_pool.tile([P, 4 * 512], BF16, name="grouped", align_bytes=64)
+                grp[(a[0], a[1])] = t_g
+                nc.scalar.copy(out=t_g[:, 0:2], in_=stg[(a[2], a[3])][:, 0:2])
             elif k == "spin":
                 s, layer, e = a
                 nc.scalar.copy(out=xg[s][:, 0, 2:4], in_=grp[(layer, e)][:, 0:2])
@@ -146,8 +166,10 @@ def tile_routed_moe_kernel(tc, xT, w1, w2, gate, offs, out):
             elif k == "i":
                 layer, e, eng = a[0], a[1], a[2]
                 parts = a[3] if len(a) > 3 else 1
-                t_g = wg_pool.tile([P, 4 * 512], BF16, name="grouped", align_bytes=64)
-                grp[(layer, e)] = t_g
+                if (layer, e) not in grp:
+                    t_g = wg_pool.tile([P, 4 * 512], BF16, name="grouped", align_bytes=64)
+                    grp[(layer, e)] = t_g
+                t_g = grp[(layer, e)]
                 raw = wraw[(layer, e)]
                 for part in range(parts):
                     if eng == "G":

@@ -22,13 +22,13 @@ HALF = 128
 NB = N // P
 STEPS = """
 lx,0,0,2 lx,0,2 lx,0,3 of lx,1,0,2 lx,1,2 lx,1,3 lw,1,0 lw,2,0 lw,1,1,lent lg,0,8 lw,2,1 r,0,0,V r,0,1,V r,0,2,V r,0,3,V r,1,0,S
-r,1,1,G r,1,2,S r,1,3,S g,0,0 g,0,1 g,0,2 g,0,3 g,0,4 g,1,0 q,0 i,1,0,S k,1,0 i,2,0,S k,2,0 i,1,1,S k,1,1 i,2,1,V k,2,1 pin,4,1,1
-f,0,0 f,0,1 h,0 g,1,1 q,1 g,1,2 q,2 f,1,0 f,1,1 h,1 s,0,0 lw,1,2 lw,2,2 i,1,2,S k,1,2 s,0,1,1,2,0 i,2,2,S k,2,2 t,0,0 t,0,1 t,0,2
-t,0,3 f,2,0 f,2,1 h,2 s,1,0 s,1,1 lw,1,3 lw,2,3 i,1,3,S k,1,3 i,2,3,S k,2,3 t,1,0 t,1,1 t,1,2 t,1,3 g,1,3 q,3 f,3,0 f,3,1 h,3
-s,2,0 s,2,1 lw,1,4 lw,2,4 i,1,4,S k,1,4 i,2,4,S k,2,4 t,2,0 t,2,1 t,2,2 t,2,3 f,4,0 f,4,1 h,4 s,3,0 s,3,1 lw,1,5 lw,2,5 i,1,5,S
-k,1,5 i,2,5,S k,2,5 t,3,0 t,3,1 t,3,2 t,3,3 g,1,4 q,4 f,5,0 f,5,1 h,5 s,4,0 s,4,1 lw,1,6 lw,2,6 i,1,6,S k,1,6 i,2,6,S k,2,6 t,4,0
-t,4,1 t,4,2 t,4,3 f,6,0 f,6,1 h,6 s,5,0 s,5,1 lw,1,7 lw,2,7 i,1,7,S k,1,7 i,2,7,S k,2,7 t,5,0 t,5,1 t,5,2 t,5,3 f,7,0 f,7,1 h,7
-s,6,0 s,7,0 m,2 m,3 t,6,0 t,6,1 t,7,0 o,0 t,7,1 o,1 t,-1,2 o,2 t,-1,3 o,3
+r,1,1,G r,1,2,S r,1,3,S g,0,0 g,0,1 gc,0,2 gc,0,3 gc,0,4 g,1,0 q,0 i,1,0,S k,1,0 i,2,0,S k,2,0 i,1,1,S k,1,1 i,2,1,V k,2,1 f,0,0
+f,0,1 h,0 g,1,1 q,1 gc,1,2 ic,2,V q,2 f,1,0 f,1,1 h,1 s,0,0 lw,1,2 lw,2,2 i,1,2,S k,1,2 s,0,1,1,2,0 i,2,2,S k,2,2 t,0,0 t,0,1
+t,0,2 t,0,3 f,2,0 f,2,1 h,2 s,1,0 s,1,1 lw,1,3 lw,2,3 i,1,3,S k,1,3 i,2,3,S k,2,3 t,1,0 t,1,1 t,1,2 t,1,3 gc,1,3 ic,3,V q,3 f,3,0
+f,3,1 h,3 s,2,0 s,2,1 lw,1,4 lw,2,4 i,1,4,S k,1,4 i,2,4,S k,2,4 t,2,0 t,2,1 t,2,2 t,2,3 f,4,0 f,4,1 h,4 s,3,0 s,3,1 lw,1,5 lw,2,5
+i,1,5,S k,1,5 i,2,5,S k,2,5 t,3,0 t,3,1 t,3,2 t,3,3 gc,1,4 ic,4,V q,4 f,5,0 f,5,1 h,5 s,4,0 s,4,1 lw,1,6 lw,2,6 i,1,6,S k,1,6
+i,2,6,S k,2,6 t,4,0 t,4,1 t,4,2 t,4,3 f,6,0 f,6,1 h,6 s,5,0 s,5,1 lw,1,7 lw,2,7 i,1,7,S k,1,7 i,2,7,S k,2,7 t,5,0 t,5,1 t,5,2
+t,5,3 f,7,0 f,7,1 h,7 s,6,0 s,7,0 m,2 m,3 t,6,0 t,6,1 t,7,0 o,0 t,7,1 o,1 t,-1,2 o,2 t,-1,3 o,3
 """
 
 
@@ -41,7 +41,7 @@ def tile_routed_moe_kernel(tc, xT, w1, w2, gate, offs, out):
         wq_pool = ctx.enter_context(tc.tile_pool(name="wq_pool", bufs=3))
         h_pool = ctx.enter_context(tc.tile_pool(name="h_pool", bufs=3))
         y_pool = ctx.enter_context(tc.tile_pool(name="y_pool", bufs=3))
-        flat_pool = ctx.enter_context(tc.tile_pool(name="flat_pool", bufs=2))
+        flat_pool = ctx.enter_context(tc.tile_pool(name="flat_pool", bufs=1))
         xq_pool = ctx.enter_context(tc.tile_pool(name="xq_pool", bufs=5))
         ps_pool = ctx.enter_context(tc.psum_pool(name="ps_pool", bufs=2))
 
@@ -125,7 +125,7 @@ def tile_routed_moe_kernel(tc, xT, w1, w2, gate, offs, out):
                 u, s = a
                 lo, n = SLICES[s]
                 if s not in flat:
-                    t_f = flat_pool.tile([P, 2, n, 2], BF16, name="flat")
+                    t_f = flat_pool.tile([P, 2, n, 2], BF16, name="flat%d" % s)
                     flat[s] = t_f
                 window = pairs[:, u, :, :].rearrange("p n e -> p (n e)").bitcast(U32)
                 nc.vector.tensor_copy(

@@ -21,14 +21,15 @@ SLICES = ((0, 256), (256, 256), (512, 512), (1024, 512), (1536, 512))
 HALF = 128
 NB = N // P
 STEPS = """
-lx,0,0,2 lx,0,2 lx,0,3 of lx,1,0,2 lx,1,2 lx,1,3 lw,1,0 lw,2,0 lw,1,1,lent lg,0,8 lw,2,1 r,0,0,V r,0,1,V r,0,2,V r,0,3,V r,1,0,S
-r,1,1,G r,1,2,S r,1,3,S g,0,0 g,0,1 gc,0,2 gc,0,3 gc,0,4 g,1,0 q,0 i,1,0,S k,1,0 i,2,0,S k,2,0 i,1,1,S k,1,1 i,2,1,V k,2,1 f,0,0
-f,0,1 h,0 g,1,1 q,1 gc,1,2 ic,2,V q,2 f,1,0 f,1,1 h,1 s,0,0 lw,1,2 lw,2,2 i,1,2,S k,1,2 s,0,1,1,2,0 i,2,2,S k,2,2 t,0,0 t,0,1
-t,0,2 t,0,3 f,2,0 f,2,1 h,2 s,1,0 s,1,1 lw,1,3 lw,2,3 i,1,3,S k,1,3 i,2,3,S k,2,3 t,1,0 t,1,1 t,1,2 t,1,3 gc,1,3 ic,3,V q,3 f,3,0
-f,3,1 h,3 s,2,0 s,2,1 lw,1,4 lw,2,4 i,1,4,S k,1,4 i,2,4,S k,2,4 t,2,0 t,2,1 t,2,2 t,2,3 f,4,0 f,4,1 h,4 s,3,0 s,3,1 lw,1,5 lw,2,5
-i,1,5,S k,1,5 i,2,5,S k,2,5 t,3,0 t,3,1 t,3,2 t,3,3 gc,1,4 ic,4,V q,4 f,5,0 f,5,1 h,5 s,4,0 s,4,1 lw,1,6 lw,2,6 i,1,6,S k,1,6
-i,2,6,S k,2,6 t,4,0 t,4,1 t,4,2 t,4,3 f,6,0 f,6,1 h,6 s,5,0 s,5,1 lw,1,7 lw,2,7 i,1,7,S k,1,7 i,2,7,S k,2,7 t,5,0 t,5,1 t,5,2
-t,5,3 f,7,0 f,7,1 h,7 s,6,0 s,7,0 m,2 m,3 t,6,0 t,6,1 t,7,0 o,0 t,7,1 o,1 t,-1,2 o,2 t,-1,3 o,3
+lx,0,0,2 lx,0,2 lx,0,3 of lx,1,0,2 lx,1,2 lx,1,3 lw,1,0 lw,2,0 lw,1,1,lent lg,0,2 lw,2,1 lg,2,8 r,0,0,V r,0,1,V r,0,2,V r,0,3,V
+r,1,0,S r,1,1,G r,1,2,S r,1,3,S gc,0,0 gc,0,1 gc,0,2 gc,0,3 gc,0,4 gc,1,0 ic,0,V q,0 i,1,0,S k,1,0 i,2,0,S k,2,0 i,1,1,S k,1,1
+i,2,1,S k,2,1 pinf,1,3,2,0 pinf,1,4,1,1 f,0,0 f,0,1 h,0 gc,1,1 ic,1,V q,1 gc,1,2 ic,2,V q,2 f,1,0 f,1,1 h,1 s,0,0 lw,1,2 lw,2,2
+i,1,2,S k,1,2 s,0,1,1,2,0 i,2,2,S k,2,2 t,0,0 t,0,1 t,0,2 t,0,3 f,2,0 f,2,1 h,2 s,1,0 s,1,1 lw,1,3 lw,2,3 i,1,3,S k,1,3 i,2,3,S
+k,2,3 t,1,0 t,1,1 t,1,2 t,1,3 gc,1,3 ic,3,V q,3 f,3,0 f,3,1 h,3 s,2,0 s,2,1 lw,1,4 lw,2,4 i,1,4,S k,1,4 i,2,4,S k,2,4 t,2,0 t,2,1
+t,2,2 t,2,3 f,4,0 f,4,1 h,4 s,3,0 s,3,1 lw,1,5 lw,2,5 i,1,5,S k,1,5 i,2,5,S k,2,5 t,3,0 t,3,1 t,3,2 t,3,3 gc,1,4 ic,4,V q,4 f,5,0
+f,5,1 h,5 s,4,0 s,4,1 lw,1,6 lw,2,6 i,1,6,S k,1,6 i,2,6,S k,2,6 t,4,0 t,4,1 t,4,2 t,4,3 f,6,0 f,6,1 h,6 s,5,0 s,5,1 lw,1,7 lw,2,7
+i,1,7,S k,1,7 i,2,7,S k,2,7 t,5,0 t,5,1 t,5,2 t,5,3 f,7,0 f,7,1 h,7 s,6,0 s,7,0 m,2 m,3 t,6,0 t,6,1 t,7,0 o,0 t,7,1 o,1 t,-1,2
+o,2 t,-1,3 o,3
 """
 
 
@@ -132,6 +133,12 @@ def tile_routed_moe_kernel(tc, xT, w1, w2, gate, offs, out):
                     out=flat[s][:, u, :, :].rearrange("p n e -> p (n e)").bitcast(U32),
                     in_=window.indirect(offsets[:, lo // 16 : (lo + n) // 16]),
                 )
+            elif k == "pinf":
+                u, s, layer, e = a
+                if s not in flat:
+                    t_f = flat_pool.tile([P, 2, SLICES[s][1], 2], BF16, name="flat%d" % s)
+                    flat[s] = t_f
+                nc.vector.tensor_copy(out=flat[s][:, u, 0, :], in_=grp[(layer, e)][:, 0:2])
             elif k == "ic":
                 s, eng = a
                 cast(eng, xg[s][:].rearrange("p n (u e) -> p n u e", u=2), flat[s][:].rearrange("p u n e -> p n u e"))

@@ -23,13 +23,13 @@ NB = N // P
 STEPS = """
 lx,0,0,2 lx,0,2 lx,0,3 of lx,1,0,2 lx,1,2 lx,1,3 lw,1,0 lw,2,0 lw,1,1,lent lg,0,2 lw,2,1 lg,2,8 r,0,0,V r,0,1,V r,0,2,V r,0,3,V
 r,1,0,S r,1,1,G r,1,2,S r,1,3,S gc,0,0 gc,0,1 gc,0,2 gc,0,3 gc,0,4 gc,1,0 ic,0,V q,0 i,1,0,S k,1,0 i,2,0,S k,2,0 i,1,1,S k,1,1
-i,2,1,S k,2,1 pinf,1,3,2,0 pinf,1,4,1,1 f,0,0 f,0,1 h,0 gc,1,1 ic,1,V q,1 gc,1,2 ic,2,V q,2 f,1,0 f,1,1 h,1 s,0,0 lw,1,2 lw,2,2
-i,1,2,S k,1,2 s,0,1,1,2,0 i,2,2,S k,2,2 t,0,0 t,0,1 t,0,2 t,0,3 f,2,0 f,2,1 h,2 s,1,0 s,1,1 lw,1,3 lw,2,3 i,1,3,S k,1,3 i,2,3,S
-k,2,3 t,1,0 t,1,1 t,1,2 t,1,3 gc,1,3 ic,3,V q,3 f,3,0 f,3,1 h,3 s,2,0 s,2,1 lw,1,4 lw,2,4 i,1,4,S k,1,4 i,2,4,S k,2,4 t,2,0 t,2,1
-t,2,2 t,2,3 f,4,0 f,4,1 h,4 s,3,0 s,3,1 lw,1,5 lw,2,5 i,1,5,S k,1,5 i,2,5,S k,2,5 t,3,0 t,3,1 t,3,2 t,3,3 gc,1,4 ic,4,V q,4 f,5,0
-f,5,1 h,5 s,4,0 s,4,1 lw,1,6 lw,2,6 i,1,6,S k,1,6 i,2,6,S k,2,6 t,4,0 t,4,1 t,4,2 t,4,3 f,6,0 f,6,1 h,6 s,5,0 s,5,1 lw,1,7 lw,2,7
-i,1,7,S k,1,7 i,2,7,S k,2,7 t,5,0 t,5,1 t,5,2 t,5,3 f,7,0 f,7,1 h,7 s,6,0 s,7,0 m,2 m,3 t,6,0 t,6,1 t,7,0 o,0 t,7,1 o,1 t,-1,2
-o,2 t,-1,3 o,3
+i,2,1,S k,2,1 pinS,1,3,2,0 spin,3,1,1 pinS,1,4,1,1 f,0,0 f,0,1 h,0 gc,1,1 ic,1,V q,1 gc,1,2 ic,2,V q,2 f,1,0 f,1,1 h,1 s,0,0
+lw,1,2 lw,2,2 i,1,2,S k,1,2 s,0,1,1,2,0 i,2,2,S k,2,2 t,0,0 t,0,1 t,0,2 t,0,3 f,2,0 f,2,1 h,2 s,1,0 s,1,1 lw,1,3 lw,2,3 i,1,3,S
+k,1,3 i,2,3,S k,2,3 t,1,0 t,1,1 t,1,2 t,1,3 gc,1,3 ic,3,V q,3 f,3,0 f,3,1 h,3 s,2,0 s,2,1 lw,1,4 lw,2,4 i,1,4,S k,1,4 i,2,4,S
+k,2,4 t,2,0 t,2,1 t,2,2 t,2,3 f,4,0 f,4,1 h,4 s,3,0 s,3,1 lw,1,5 lw,2,5 i,1,5,S k,1,5 i,2,5,S k,2,5 t,3,0 t,3,1 t,3,2 t,3,3
+gc,1,4 ic,4,V q,4 f,5,0 f,5,1 h,5 s,4,0 s,4,1 lw,1,6 lw,2,6 i,1,6,S k,1,6 i,2,6,S k,2,6 t,4,0 t,4,1 t,4,2 t,4,3 f,6,0 f,6,1 h,6
+s,5,0 s,5,1 lw,1,7 lw,2,7 i,1,7,S k,1,7 i,2,7,S k,2,7 t,5,0 t,5,1 t,5,2 t,5,3 f,7,0 f,7,1 h,7 s,6,0 s,7,0 m,2 m,3 t,6,0 t,6,1
+t,7,0 o,0 t,7,1 o,1 t,-1,2 o,2 t,-1,3 o,3
 """
 
 
@@ -133,12 +133,12 @@ def tile_routed_moe_kernel(tc, xT, w1, w2, gate, offs, out):
                     out=flat[s][:, u, :, :].rearrange("p n e -> p (n e)").bitcast(U32),
                     in_=window.indirect(offsets[:, lo // 16 : (lo + n) // 16]),
                 )
-            elif k == "pinf":
+            elif k == "pinf" or k == "pinS":
                 u, s, layer, e = a
                 if s not in flat:
                     t_f = flat_pool.tile([P, 2, SLICES[s][1], 2], BF16, name="flat%d" % s)
                     flat[s] = t_f
-                nc.vector.tensor_copy(out=flat[s][:, u, 0, :], in_=grp[(layer, e)][:, 0:2])
+                cast("V" if k == "pinf" else "S", flat[s][:, u, 0, :], grp[(layer, e)][:, 0:2])
             elif k == "ic":
                 s, eng = a
                 cast(eng, xg[s][:].rearrange("p n (u e) -> p n u e", u=2), flat[s][:].rearrange("p u n e -> p n u e"))

from contextlib import ExitStack

import concourse.mybir as mybir

K, T, E, C, H, N = 512, 2048, 8, 256, 512, 512
FLOPS = 2 * E * C * (K * H + H * N)

F32 = mybir.dt.float32
BF16 = mybir.dt.bfloat16
U32 = mybir.dt.uint32
U16 = mybir.dt.uint16
U8 = mybir.dt.uint8
FP8X4 = mybir.dt.float8_e4m3fn_x4
SILU = mybir.ActivationFunctionType.Silu
MULT = mybir.AluOpType.mult

NUMS = tuple(str(v) for v in range(-1, 64))
P = 128
XW = 512
SLICES = ((0, 256), (256, 256), (512, 512), (1024, 512), (1536, 512))
HALF = 128
NB = N // P
STEPS = """
lx,0,0,2 lx,0,2 lx,0,3 of lx,1,0,2 lx,1,2 lx,1,3 lw,1,0 lw,2,0 lw,1,1,lent lg,0,2 lw,2,1 lg,2,8 r,0,0,V r,0,1,V r,0,2,V r,0,3,V
r,1,0,S r,1,1,G r,1,2,S r,1,3,S gc,0,0 gc,0,1 gc,0,2 gc,0,3 gc,0,4 gc,1,0 ic,0,V q,0 i,1,0,S k,1,0 i,2,0,S k,2,0 i,1,1,S k,1,1
i,2,1,S k,2,1 pinS,1,3,2,0 spin,3,1,1 pinS,1,4,1,1 f,0,0 f,0,1 h,0 gc,1,1 ic,1,V q,1 gc,1,2 ic,2,V q,2 f,1,0 f,1,1 h,1 s,0,0
lw,1,2 lw,2,2 i,1,2,S k,1,2 s,0,1,1,2,0 i,2,2,S k,2,2 t,0,0 t,0,1 t,0,2 t,0,3 f,2,0 f,2,1 h,2 s,1,0 s,1,1 lw,1,3 lw,2,3 i,1,3,S
k,1,3 i,2,3,S k,2,3 t,1,0 t,1,1 t,1,2 t,1,3 gc,1,3 ic,3,V q,3 f,3,0 f,3,1 h,3 s,2,0 s,2,1 lw,1,4 lw,2,4 i,1,4,S k,1,4 i,2,4,S
k,2,4 t,2,0 t,2,1 t,2,2 t,2,3 f,4,0 f,4,1 h,4 s,3,0 s,3,1 lw,1,5 lw,2,5 i,1,5,S k,1,5 i,2,5,S k,2,5 t,3,0 t,3,1 t,3,2 t,3,3
gc,1,4 ic,4,V q,4 f,5,0 f,5,1 h,5 s,4,0 s,4,1 lw,1,6 lw,2,6 i,1,6,S k,1,6 i,2,6,S k,2,6 t,4,0 t,4,1 t,4,2 t,4,3 f,6,0 f,6,1 h,6
s,5,0 s,5,1 lw,1,7 lw,2,7 i,1,7,S k,1,7 i,2,7,S k,2,7 t,5,0 t,5,1 t,5,2 t,5,3 f,7,0 f,7,1 h,7 s,6,0 s,7,0 m,2 m,3 t,6,0 t,6,1
t,7,0 o,0 t,7,1 o,1 t,-1,2 o,2 t,-1,3 o,3
"""


def tile_routed_moe_kernel(tc, xT, w1, w2, gate, offs, out):
    nc = tc.nc
    with ExitStack() as ctx:
        keep = ctx.enter_context(tc.tile_pool(name="keep", bufs=1))
        wraw_pool = ctx.enter_context(tc.tile_pool(name="wraw_pool", bufs=5))
        wg_pool = ctx.enter_context(tc.tile_pool(name="wg_pool", bufs=3))
        wq_pool = ctx.enter_context(tc.tile_pool(name="wq_pool", bufs=3))
        h_pool = ctx.enter_context(tc.tile_pool(name="h_pool", bufs=3))
        y_pool = ctx.enter_context(tc.tile_pool(name="y_pool", bufs=3))
        flat_pool = ctx.enter_context(tc.tile_pool(name="flat_pool", bufs=1))
        xq_pool = ctx.enter_context(tc.tile_pool(name="xq_pool", bufs=5))
        ps_pool = ctx.enter_context(tc.psum_pool(name="ps_pool", bufs=2))

        offsets = keep.tile([P, E * C // 16], U16, name="offsets")
        warm_in = keep.tile([P, 1], F32, name="warm_in")
        warm_out = keep.tile([P, 1], F32, name="warm_out")
        nc.gpsimd.memset(warm_in[:], 0.0)
        nc.scalar.activation(out=warm_out[:], in_=warm_in[:], func=SILU)

        x_view = xT.rearrange("(p t) n -> p t n", t=4)
        gate_sb = keep.tile([P, E * C], F32, name="gate_sb")
        pairs = keep.tile([P, 2, T, 2], BF16, name="pairs")
        out_sb = [keep.tile([P, T], F32, name="out_sb%d" % nb) for nb in range(NB)]
        xg = [keep.tile([P, n, 4], BF16, name="xg%d" % s, align_bytes=64) for s, (lo, n) in enumerate(SLICES)]
        xraw = {}
        planes = {}
        flat = {}
        wraw = {}
        grp = {}
        wq = {}
        xq = {}
        hg = {}
        hq = {}
        y = {}
        stg = {}
        stamp = keep.tile([P, 8], U32, name="stamp")
        n_stamp = 0

        def cast(eng, dst, src):
            if eng == "V":
                nc.vector.tensor_copy(out=dst, in_=src)
            elif eng == "S":
                nc.scalar.copy(out=dst, in_=src)
            else:
                nc.gpsimd.tensor_scalar(dst, src, 1.0, 0.0, MULT, mybir.AluOpType.add)

        def y_plane(e, b):
            if e not in y:
                tile_y = y_pool.tile([P, NB, C], F32, name="y")
                y[e] = tile_y
            return y[e][:, 2 * b : 2 * b + 2, :]

        for step in STEPS.split():
            op = step.split(",")
            k = op[0]
            a = [int(v) if v.replace("-", "") in NUMS else v for v in op[1:]]
            if k == "of":
                nc.sync.dma_start(offsets[:], offs)
            elif k == "lx":
                u, c = a[0], a[1]
                n = a[2] if len(a) > 2 else 1
                t_x = keep.tile([P, 2, n * XW], F32, name="xraw%d_%d" % (u, c))
                nc.sync.dma_start(out=t_x[:], in_=x_view[:, 2 * u : 2 * u + 2, c * XW : (c + n) * XW])
                for i in range(n):
                    xraw[(u, c + i)] = t_x[:, :, i * XW : (i + 1) * XW]
            elif k == "lw":
                layer, e = a[0], a[1]
                w = w1 if layer == 1 else w2
                if len(a) > 2:
                    t_b = wraw_pool.tile([P, 2 * 4 * 512], BF16, name="wraw", align_bytes=64)
                    hg[0] = t_b[:, 0 : 4 * C].rearrange("p (n t) -> p n t", t=4)
                    wraw[(layer, e)] = t_b[:].bitcast(F32).rearrange("p (j c) -> p j c", j=4)
                else:
                    t_w = wraw_pool.tile([P, 4, 512], F32, name="wraw", align_bytes=64)
                    wraw[(layer, e)] = t_w[:]
                nc.sync.dma_start(out=wraw[(layer, e)], in_=w[e, :, :].rearrange("(p j) c -> p j c", j=4))
            elif k == "lg":
                lo, hi = a[0] * C, a[1] * C
                nc.sync.dma_start(out=gate_sb[:, lo:hi], in_=gate[0:P, lo:hi])
            elif k == "r":
                u, c, eng = a[0], a[1], a[2]
                lo, hi = (a[3] * 128, a[4] * 128) if len(a) > 3 else (0, XW)
                cast(eng, pairs[:, u, c * XW + lo : c * XW + hi, :], xraw[(u, c)][:, :, lo:hi].rearrange("p e n -> p n e"))
            elif k == "g":
                u, s = a
                lo, n = SLICES[s]
                window = pairs[:, u, :, :].rearrange("p n e -> p (n e)").bitcast(U32)
                words = xg[s][:].rearrange("p n t -> p (n t)").bitcast(U32).rearrange("p (n u) -> p n u", u=2)
                nc.vector.tensor_copy(out=words[:, :, u], in_=window.indirect(offsets[:, lo // 16 : (lo + n) // 16]))
            elif k == "gc":
                u, s = a
                lo, n = SLICES[s]
                if s not in flat:
                    t_f = flat_pool.tile([P, 2, n, 2], BF16, name="flat%d" % s)
                    flat[s] = t_f
                window = pairs[:, u, :, :].rearrange("p n e -> p (n e)").bitcast(U32)
                nc.vector.tensor_copy(
                    out=flat[s][:, u, :, :].rearrange("p n e -> p (n e)").bitcast(U32),
                    in_=window.indirect(offsets[:, lo // 16 : (lo + n) // 16]),
                )
            elif k == "pinf" or k == "pinS":
                u, s, layer, e = a
                if s not in flat:
                    t_f = flat_pool.tile([P, 2, SLICES[s][1], 2], BF16, name="flat%d" % s)
                    flat[s] = t_f
                cast("V" if k == "pinf" else "S", flat[s][:, u, 0, :], grp[(layer, e)][:, 0:2])
            elif k == "ic":
                s, eng = a
                cast(eng, xg[s][:].rearrange("p n (u e) -> p n u e", u=2), flat[s][:].rearrange("p u n e -> p n u e"))
            elif k == "c":
                t, c, eng = a
                if t not in planes:
                    t_p = keep.tile([P, T], BF16, name="plane%d" % t)
                    planes[t] = t_p
                cast(eng, planes[t][:, c * XW : (c + 1) * XW], xraw[(t // 2, c)][:, t % 2, :])
            elif k == "gs":
                t, s = a
                lo, n = SLICES[s]
                nc.scalar.activation(
                    out=xg[s][:, :, t],
                    in_=planes[t][:].indirect(offsets[:, lo // 16 : (lo + n) // 16]),
                    func=mybir.ActivationFunctionType.Copy,
                )
            elif k == "pg":
                t_g = wg_pool.tile([P, 4 * 512], BF16, name="grouped", align_bytes=64)
                grp[(a[0], a[1])] = t_g
                nc.scalar.copy(out=t_g[:, 0:2], in_=stg[(a[2], a[3])][:, 0:2])
            elif k == "spin":
                s, layer, e = a
                nc.scalar.copy(out=xg[s][:, 0, 2:4], in_=grp[(layer, e)][:, 0:2])
            elif k == "q":
                s = a[0]
                n = SLICES[s][1]
                xc = xq_pool.tile([P, n], U32, name="xc", align_bytes=64)
                xs = xq_pool.tile([P, n], U8, name="xs", align_bytes=64)
                xq[s] = (xc, xs)
                nc.vector.quantize_mx(out=xc[:].bitcast(FP8X4), scales=xs[:], in_=xg[s][:].rearrange("p n t -> p (n t)"))
            elif k == "i":
                layer, e, eng = a[0], a[1], a[2]
                parts = a[3] if len(a) > 3 else 1
                if (layer, e) not in grp:
                    t_g = wg_pool.tile([P, 4 * 512], BF16, name="grouped", align_bytes=64)
                    grp[(layer, e)] = t_g
                t_g = grp[(layer, e)]
                raw = wraw[(layer, e)]
                for part in range(parts):
                    if eng == "G":
                        w = 512 // parts
                        if layer == 2:
                            dst = t_g[:, 4 * w * part : 4 * w * (part + 1)].rearrange("p (c j) -> p c j", j=4)
                            src = raw[:, :, w * part : w * (part + 1)].rearrange("p j c -> p c j")
                        else:
                            mm = 128 // parts
                            dst = t_g[:].rearrange("p (t m j) -> p t m j", t=4, j=4)[:, :, mm * part : mm * (part + 1), :]
                            src = raw.rearrange("p j (m t) -> p t m j", t=4)[:, :, mm * part : mm * (part + 1), :]
                    elif layer == 1:
                        dst = t_g[:].rearrange("p (t m j) -> p m j t", t=4, j=4)
                        src = raw.rearrange("p j (m t) -> p m j t", t=4)
                    else:
                        dst = t_g[:].rearrange("p (c i j) -> p c j i", i=4, j=4)
                        src = raw.rearrange("p j (c i) -> p c j i", i=4)
                    cast(eng, dst, src)
            elif k == "k":
                layer, e = a
                codes = wq_pool.tile([P, 512], U32, name="codes%d" % layer, align_bytes=64)
                scales = wq_pool.tile([P, 512], U8, name="scales%d" % layer, align_bytes=64)
                wq[(layer, e)] = (codes, scales)
                nc.vector.quantize_mx(out=codes[:].bitcast(FP8X4), scales=scales[:], in_=grp[(layer, e)][:])
            elif k == "pin":
                s, layer, e = a
                nc.vector.tensor_copy(out=xg[s][:, 0, 2:4], in_=grp[(layer, e)][:, 0:2])
            elif k == "pin0":
                s, layer, e = a
                nc.vector.tensor_copy(out=xg[s][:, 0, 0:2], in_=grp[(layer, e)][:, 0:2])
            elif k == "f":
                e, half = a
                s = [i for i, (lo, n) in enumerate(SLICES) if lo <= e * C < lo + n][0]
                lo = e * C - SLICES[s][0] + half * HALF
                c1, s1 = wq[(1, e)]
                xc, xs = xq[s]
                if e not in hg:
                    t_h = h_pool.tile([P, C, 4], BF16, name="hg", align_bytes=64)
                    hg[e] = t_h[:]
                ps1 = ps_pool.tile([P, 4, HALF], F32, name="bank")
                for t in range(4):
                    nc.tensor.matmul_mx(
                        out=ps1[:, t, :],
                        lhsT=c1[:, t * P : (t + 1) * P].bitcast(FP8X4),
                        lhsT_scale=s1[:, t * P : (t + 1) * P],
                        rhs=xc[:, lo : lo + HALF].bitcast(FP8X4),
                        rhs_scale=xs[:, lo : lo + HALF],
                        start=True,
                        stop=True,
                    )
                nc.scalar.activation(out=hg[e][:, half * HALF : (half + 1) * HALF, :], in_=ps1[:].rearrange("p t n -> p n t"), func=SILU)
            elif k == "h":
                e = a[0]
                hc = h_pool.tile([P, C], U32, name="hc", align_bytes=64)
                hs = h_pool.tile([P, C], U8, name="hs", align_bytes=64)
                hq[e] = (hc, hs)
                nc.vector.quantize_mx(out=hc[:].bitcast(FP8X4), scales=hs[:], in_=hg[e].rearrange("p n t -> p (n t)"))
            elif k == "s" or k == "m":
                if k == "s":
                    e, b = a[0], a[1]
                    blocks = ((e, 2 * b), (e, 2 * b + 1))
                    if len(a) > 2:
                        plane = wraw[(a[2], a[3])][:, a[4], :].rearrange("p (a c) -> p a c", a=2)
                    else:
                        plane = y_plane(e, b)
                    stg[(e, 2 * b)] = plane[:, 0, :]
                    stg[(e, 2 * b + 1)] = plane[:, 1, :]
                else:
                    nb = a[0]
                    blocks = ((E - 2, nb), (E - 1, nb))
                    plane = y_plane(E - 4 + nb, 1)
                    stg[(-1, nb)] = plane.rearrange("p a c -> p (a c)")
                ps2 = ps_pool.tile([P, 2, C], F32, name="bank")
                for i, (e, nb) in enumerate(blocks):
                    c2, s2 = wq[(2, e)]
                    hc, hs = hq[e]
                    nc.tensor.matmul_mx(
                        out=ps2[:, i, :],
                        lhsT=c2[:, nb * P : (nb + 1) * P].bitcast(FP8X4),
                        lhsT_scale=s2[:, nb * P : (nb + 1) * P],
                        rhs=hc[:].bitcast(FP8X4),
                        rhs_scale=hs[:],
                        start=True,
                        stop=True,
                    )
                nc.scalar.copy(out=plane, in_=ps2[:])
            elif k == "t":
                e, nb = a
                lo, hi = (e * C, (e + 1) * C) if e >= 0 else ((E - 2) * C, E * C)
                window = out_sb[nb][:].indirect(offsets[:, lo // 16 : hi // 16])
                nc.vector.tensor_tensor(window, stg[(e, nb)], gate_sb[:, lo:hi], MULT)
            elif k == "o":
                nb = a[0]
                nc.sync.dma_start(out=out[nb * P : (nb + 1) * P, :], in_=out_sb[nb][:])
            elif k == "z":
                what = a[0]
                if what == "h":
                    probe = hq[a[1]][0][:, 0:1]
                elif what == "y":
                    probe = stg[(a[1], a[2])][:, 0:1].bitcast(U32)
                elif what == "g":
                    probe = grp[(a[1], a[2])][:, 0:2].bitcast(U32)
                elif what == "p":
                    probe = pairs[:, a[1], T - 1, :].bitcast(U32)
                elif what == "k":
                    probe = wq[(a[1], a[2])][0][:, 0:1]
                else:
                    probe = out_sb[a[1]][:, 0:1].bitcast(U32)
                nc.gpsimd.tensor_copy(out=stamp[:, n_stamp : n_stamp + 1], in_=probe)
                n_stamp += 1
